import numpy as np
import ml_dtypes


def mxq(x, axis, fmt="e4m3"):
    dtype, down = {"e4m3": (ml_dtypes.float8_e4m3fn, 7), "e5m2": (ml_dtypes.float8_e5m2, 14)}[fmt]
    v = np.moveaxis(np.asarray(x, np.float32).astype(ml_dtypes.bfloat16).astype(np.float64), axis, -1)
    blocks = v.reshape(v.shape[:-1] + (-1, 32))
    amax = np.abs(blocks).max(-1, keepdims=True)
    byte = np.maximum(np.where(amax > 0, np.frexp(amax)[1] - 1 + 127, 0) - down, 1)
    scale = np.exp2(byte - 127.0)
    codes = (blocks / scale).astype(np.float32).astype(dtype).astype(np.float64)
    return np.moveaxis((codes * scale).reshape(v.shape), -1, axis)


WIDE = False


def mx_kscale(k):
    if not WIDE:
        return np.ones(k)
    levels = np.array([18, -18])
    if k % 512:
        return np.exp2(np.random.permutation(np.resize(levels, k // 32))).repeat(32)
    a = np.empty((k // 512, 16))
    for p in range(k // 512):
        a[p, :8] = np.random.permutation(np.resize(levels, 8))
        for g in range(8):
            far = levels[np.abs(levels - a[p, g]) >= 10]
            a[p, g + 8] = far[np.random.randint(len(far))]
    return np.exp2(a.ravel()).repeat(32)


def f64(x):
    return np.asarray(x).astype(np.float64)


def striped(idx):
    return np.tile(np.asarray(idx).reshape(-1, 16).T, (8, 1)).astype(np.uint16)


def unstriped(offs):
    return offs[:16].T.reshape(-1).astype(np.int64)


B, N, T, D, DV, R = 1, 512, 2048, 512, 512, 1024


def setup_inputs():
    n = np.random.standard_normal
    idx = np.random.permutation(T)[:B * N]
    s = mx_kscale(D)[:, None]
    v = mx_kscale(DV)[:, None]
    q = n((B, D, R))
    do = n((B, DV, R))
    u = np.ones(T)
    u[idx] = mx_kscale(B * N)
    r = np.random.uniform(0.5, 2.0, T) * u
    return {
        "qT": (q * s).astype(np.float32),
        "kT": (n((D, T)) * (0.50 / np.sqrt(D)) / s / r).astype(np.float32),
        "vT": (n((DV, T)) / np.sqrt(DV) / v).astype(np.float32),
        "doT": (do * v).astype(np.float32),
        "lse": (np.log(N) + 0.12 + 0.1 * n((B, R, 1))).astype(np.float32),
        "delta": (0.3 * n((B, R, 1))).astype(np.float32),
        "rw": (np.random.uniform(0.5, 1.5, (B, R, 1)) * N / np.sqrt(R)).astype(np.float32),
        "ts": np.tile(r, (128, 1)).astype(np.float32),
        "offs": striped(idx),
    }


def reference(qT, kT, vT, doT, lse, delta, rw, ts, offs):
    idx = unstriped(offs)
    pick = lambda x: x[:, idx].reshape(x.shape[0], B, N).transpose(1, 0, 2)
    k = pick(f64(kT))
    a = mxq(f64(qT), 1, "e4m3").transpose(0, 2, 1) @ mxq(k, 1, "e4m3")
    ts_ = pick(f64(ts))[:, :1, :]
    a = a * ts_
    p = np.exp(a - f64(lse))
    dp = mxq(f64(doT), 1, "e5m2").transpose(0, 2, 1) @ mxq(pick(f64(vT)), 1, "e4m3")
    ds = f64(rw) * p * (dp - f64(delta))
    ds = ts_ * ds
    gq = mxq(ds, 2, "e5m2") @ mxq(k, 2, "e4m3").transpose(0, 2, 1)
    return gq

@@ -1,0 +1,251 @@
+from contextlib import ExitStack
+
+import concourse.mybir as mybir
+from concourse.masks import make_identity
+
+N, T, D, DV, R = 512, 2048, 512, 512, 1024
+FLOPS = 2 * R * N * (D + DV + D)
+
+F32 = mybir.dt.float32
+BF16 = mybir.dt.bfloat16
+U32 = mybir.dt.uint32
+U16 = mybir.dt.uint16
+U8 = mybir.dt.uint8
+E4M3 = mybir.dt.float8_e4m3fn_x4
+E5M2 = mybir.dt.float8_e5m2_x4
+ALU = mybir.AluOpType
+ACT = mybir.ActivationFunctionType
+
+P = 128
+PACK = 4
+TILES = R // P
+Q_CHUNKS = (256, 256, 512)
+DO_CHUNK = 256
+
+
+def tile_attend_gat_lse_q_ts_kernel(tc, qT, kT, vT, doT, lse, delta, rw, ts, offs, out):
+    nc = tc.nc
+    with ExitStack() as ctx:
+        keep = ctx.enter_context(tc.tile_pool(name="keep", bufs=1))
+        ring = ctx.enter_context(tc.tile_pool(name="ring", bufs=4))
+        psum = ctx.enter_context(tc.psum_pool(name="psum", bufs=1))
+
+        def bank(tag, name):
+            return psum.tile([P, 512], F32, name=name, tag=tag, bufs={"A": 3, "B": 2, "C": 3}[tag])
+
+        def quantize(src, width, fmt, name, pool=keep, tag=None):
+            codes = pool.tile([P, width], U32, name=name + "_codes", tag=(tag or name) + "_codes", align_bytes=64)
+            scales = pool.tile([P, width], U8, name=name + "_scales", tag=(tag or name) + "_scales", align_bytes=64)
+            nc.vector.quantize_mx(out=codes[:].bitcast(fmt), scales=scales[:], in_=src)
+            return codes, scales
+
+        def interleave(engine, raw, width, name, tag):
+            grouped = keep.tile([P, width * PACK], BF16, name=name, tag=tag, align_bytes=64)
+            dst = grouped[:].rearrange("p (c i j) -> p c j i", i=4, j=PACK)
+            src = raw[:].rearrange("p j (c i) -> p c j i", i=4)
+            if engine == "vector":
+                nc.vector.tensor_copy(out=dst, in_=src)
+            else:
+                nc.scalar.copy(out=dst, in_=src)
+            return grouped
+
+        offsets = keep.tile([P, N // 16], U16, name="offsets")
+        nc.sync.dma_start(offsets[:], offs)
+
+        rows = keep.tile([P, P], F32, name="rows")
+        nc.gpsimd.memset(rows[:], 0.0)
+        ts_pool = keep.tile([P, T], F32, name="ts_pool")
+        nc.vector.memset(ts_pool[32:64, :], 0.0)
+        nc.vector.memset(ts_pool[64:128, :], 0.0)
+        ident = keep.tile([P, P], F32, name="ident")
+        make_identity(nc, ident[:])
+        nc.sync.dma_start(out=ts_pool[0:32, :], in_=ts[0:32, :])
+        for n, vec in enumerate((rw, lse, delta)):
+            nc.scalar.dma_start(out=rows[TILES * n : TILES * (n + 1), :], in_=vec[0].rearrange("(i m) o -> i (m o)", m=P))
+
+        q_view = qT[0].rearrange("(p j) r -> p j r", j=PACK)
+        do_view = doT[0].rearrange("(p j) r -> p j r", j=PACK)
+        k_view = kT.rearrange("(p j) t -> p j t", j=PACK)
+        v_view = vT.rearrange("(p j) t -> p j t", j=PACK)
+
+        def load(view, name, tag):
+            raw = keep.tile(list(view.shape), F32, name=name, tag=tag)
+            nc.sync.dma_start(out=raw[:], in_=view)
+            return raw
+
+        q_starts = [sum(Q_CHUNKS[:c]) for c in range(len(Q_CHUNKS))]
+        k_pool = [load(k_view[:, j, :], "k_pool%d" % j, "plane%d" % j) for j in range(PACK)]
+        q_raw = [load(q_view[:, :, a : a + w], "q_raw%d" % a, "q_raw%d" % a) for a, w in zip(q_starts, Q_CHUNKS)]
+
+        ts_row = keep.tile([P, N], F32, name="ts_row")
+        nc.vector.tensor_copy(out=ts_row[:], in_=ts_pool[:].indirect(offsets[:]))
+        ts_by_block = bank("B", "ts_by_block")
+        ts_by_place = bank("B", "ts_by_place")
+        rows_t = bank("C", "rows_t")
+        for j in range(PACK):
+            nc.tensor.transpose(ts_by_block[:, j * P : (j + 1) * P], ts_row[:, j * P : (j + 1) * P], ident[:])
+        for t in range(PACK):
+            nc.tensor.transpose(ts_by_place[:, t * P : (t + 1) * P], ts_row[:, t:N:PACK], ident[:])
+        nc.tensor.transpose(rows_t[:, 0:P], rows[:], ident[:])
+        cols = keep.tile([P, 32], F32, name="cols")
+        nc.scalar.copy(out=cols[:, 0:4], in_=ts_by_block[:, 0:N:P])
+        nc.scalar.copy(out=cols[:, 4:8], in_=ts_by_place[:, 0:N:P])
+        nc.scalar.copy(out=cols[:, 8:32], in_=rows_t[:, 0:24])
+        factors = cols[:, 0:16]
+        positive = keep.tile([P, 16], F32, name="positive")
+        nc.gpsimd.tensor_scalar(positive[:], factors, 0.0, 2.0, ALU.is_ge, ALU.mult)
+        sign = keep.tile([P, 16], F32, name="sign")
+        nc.gpsimd.tensor_scalar(sign[:], positive[:], -1.0, None, ALU.add)
+        absolute = keep.tile([P, 16], F32, name="absolute")
+        nc.gpsimd.tensor_tensor(absolute[:], factors, sign[:], ALU.mult)
+        size = keep.tile([P, 16], F32, name="size")
+        nc.gpsimd.tensor_scalar(size[:], absolute[:], 2.0**-126, None, ALU.max)
+        parts = keep.tile([P, 48], F32, name="parts", tag="first", align_bytes=64)
+        nc.gpsimd.tensor_scalar(parts[:, 0:16], size[:], 2.0**64, 2.0**-63, ALU.min, ALU.max)
+        nc.gpsimd.tensor_scalar(parts[:, 16:32], size[:], 2.0**-64, 1.0, ALU.mult, ALU.max)
+        nc.gpsimd.tensor_scalar(parts[:, 32:48], size[:], 2.0**63, 1.0, ALU.mult, ALU.min)
+        log_parts = keep.tile([P, 48], F32, name="log_parts", tag="second", align_bytes=64)
+        nc.scalar.activation(log_parts[:], parts[:], ACT.Ln)
+        log_edges = keep.tile([P, 16], F32, name="log_edges")
+        nc.gpsimd.tensor_tensor(log_edges[:], log_parts[:, 16:32], log_parts[:, 32:48], ALU.add)
+        log_size = keep.tile([P, 16], F32, name="log_size")
+        nc.gpsimd.tensor_tensor(log_size[:], log_parts[:, 0:16], log_edges[:], ALU.add)
+        exp_bias = keep.tile([P, TILES], F32, name="exp_bias")
+        nc.gpsimd.tensor_tensor(exp_bias[:], log_size[:, 8:16], cols[:, 16:24], ALU.subtract)
+
+        k_bf = keep.tile([P, N * PACK], BF16, name="k_bf", align_bytes=64)
+        for j in range(PACK):
+            nc.vector.tensor_copy(out=k_bf[:, j : N * PACK : PACK], in_=k_pool[j][:].indirect(offsets[:]))
+        k_codes, k_scales = quantize(k_bf[:], N, E4M3, "k")
+
+        weights = []
+
+        def prepare_q(c, engine, tag):
+            return quantize(interleave(engine, q_raw[c], Q_CHUNKS[c], "q_bf%d" % c, tag)[:], Q_CHUNKS[c], E4M3, "q%d" % c)
+
+        def weigh(c, q_mx):
+            q_codes, q_scales = q_mx
+            width = Q_CHUNKS[c]
+            logits = []
+            for j in range(PACK):
+                scores = bank("A", "scores")
+                nc.tensor.matmul_mx(
+                    out=scores[:, 0:width],
+                    lhsT=k_codes[:, j * P : (j + 1) * P].bitcast(E4M3),
+                    lhsT_scale=k_scales[:, j * P : (j + 1) * P],
+                    rhs=q_codes[:].bitcast(E4M3),
+                    rhs_scale=q_scales[:],
+                    start=True,
+                    stop=True,
+                )
+                logit = keep.tile([P, width], F32, name="logit%d_%d" % (c, j), tag="logit%d_%d" % (c, j), align_bytes=64)
+                nc.scalar.activation(logit[:], scores[:, 0:width], ACT.Identity, bias=log_size[:, j : j + 1], scale=cols[:, j : j + 1])
+                logits.append(logit)
+            for m in range(width // P):
+                i = q_starts[c] // P + m
+                turned = bank("C", "turned")
+                for j in range(PACK):
+                    nc.tensor.transpose(turned[:, j * P : (j + 1) * P], logits[j][:, m * P : (m + 1) * P], ident[:])
+                weight = keep.tile([P, N], F32, name="weight%d" % i, tag="weight%d" % i, align_bytes=64)
+                nc.scalar.activation(
+                    weight[:].rearrange("p (u s e) -> p u s e", u=2, e=2),
+                    turned[:].rearrange("p (s u e) -> p u s e", u=2, e=2),
+                    ACT.Exp,
+                    bias=exp_bias[:, i : i + 1],
+                )
+                weights.append(weight)
+
+        q_first = prepare_q(0, "scalar", "first")
+        q_second = prepare_q(1, "scalar", "second")
+        weigh(0, q_first)
+        weigh(1, q_second)
+
+        k_words = k_bf[:].bitcast(F32)
+        ks_bf = keep.tile([P, D * PACK], BF16, name="ks_bf", tag="wide", align_bytes=64)
+        ks_view = ks_bf[:].rearrange("s (p u e t) -> s u p e t", u=2, e=2, t=PACK)
+        for u in range(2):
+            k_turned = bank("B", "k_turned")
+            for t in range(PACK):
+                nc.tensor.transpose(k_turned[:, t * P : (t + 1) * P], k_words[:, 2 * t + u : 2 * N : 2 * PACK], ident[:])
+            nc.vector.tensor_tensor(
+                ks_view[:, u],
+                k_turned[:].bitcast(BF16).rearrange("s (t p e) -> s p e t", t=PACK, e=2),
+                sign[:, 4:8].unsqueeze(1).unsqueeze(1).to_broadcast([P, P, 2, PACK]),
+                ALU.mult,
+            )
+        ks_codes, ks_scales = quantize(ks_bf[:], D, E4M3, "ks")
+        weigh(2, prepare_q(2, "vector", "wide"))
+
+        v_pool = [load(v_view[:, j, :], "v_pool%d" % j, "plane%d" % j) for j in range(PACK)]
+        v_bf = keep.tile([P, N * PACK], BF16, name="v_bf", tag="wide", align_bytes=64)
+        v_view_bf = v_bf[:].rearrange("p (u s e j) -> p j s u e", u=2, e=2, j=PACK)
+        for j in range(PACK):
+            nc.vector.tensor_copy(out=v_view_bf[:, j], in_=v_pool[j][:].indirect(offsets[:]))
+        v_codes, v_scales = quantize(v_bf[:], N, E4M3, "v")
+
+        do_raw = [load(do_view[:, :, c * DO_CHUNK : (c + 1) * DO_CHUNK], "do_raw%d" % c, "plane%d" % c) for c in range(R // DO_CHUNK)]
+        do_tags = ("logit2_3", "wide", "weight0", "weight2")
+        do_mx = {}
+        per_chunk = DO_CHUNK // P
+
+        def prepare_do(c):
+            grouped = interleave("scalar" if c % 2 == 0 else "vector", do_raw[c], DO_CHUNK, "do_bf%d" % c, do_tags[c])
+            do_mx[c] = quantize(grouped[:], DO_CHUNK, E5M2, "do%d" % c)
+
+        dp, ds_t, ds_mx = {}, {}, {}
+
+        def multiply_values(i):
+            codes, scales = do_mx[i // per_chunk]
+            cols_i = slice((i % per_chunk) * P, (i % per_chunk + 1) * P)
+            dp[i] = bank("A", "dp")
+            nc.tensor.matmul_mx(
+                out=dp[i][:],
+                lhsT=codes[:, cols_i].bitcast(E5M2),
+                lhsT_scale=scales[:, cols_i],
+                rhs=v_codes[:].bitcast(E4M3),
+                rhs_scale=v_scales[:],
+                start=True,
+                stop=True,
+            )
+
+        def make_ds(i):
+            ds = ring.tile([P, N], BF16, name="ds", align_bytes=64)
+            nc.vector.scalar_tensor_tensor(ds[:], dp[i][:], cols[:, 24 + i : 25 + i], weights[i][:], ALU.subtract, ALU.mult)
+            ds_words = ds[:].bitcast(F32)
+            ds_turned = bank("B", "ds_turned")
+            for u in range(2):
+                nc.tensor.transpose(ds_turned[:, u * P : (u + 1) * P], ds_words[:, u * P : (u + 1) * P], ident[:])
+            ds_t[i] = ring.tile([P, N], BF16, name="ds_t", align_bytes=64)
+            nc.scalar.copy(
+                out=ds_t[i][:].bitcast(F32).rearrange("s (r u) -> s r u", u=2),
+                in_=ds_turned[:, 0 : 2 * P].rearrange("s (u r) -> s r u", u=2),
+            )
+
+        def finish(i):
+            codes, scales = quantize(ds_t[i][:], P, E5M2, "ds%d" % i, pool=ring, tag="dsq")
+            grad = bank("C", "grad")
+            nc.tensor.matmul_mx(
+                out=grad[:],
+                lhsT=codes[:].bitcast(E5M2),
+                lhsT_scale=scales[:],
+                rhs=ks_codes[:].bitcast(E4M3),
+                rhs_scale=ks_scales[:],
+                start=True,
+                stop=True,
+            )
+            result = ring.tile([P, D], F32, name="result")
+            nc.scalar.activation(result[:], grad[:], ACT.Copy, scale=sign[:, 8 + i : 9 + i])
+            nc.sync.dma_start(out=out[0, i * P : (i + 1) * P, :], in_=result[:])
+
+        prepare_do(0)
+        multiply_values(0)
+        multiply_values(1)
+        for i in range(TILES):
+            make_ds(i)
+            if i % per_chunk == 0 and i // per_chunk + 1 < R // DO_CHUNK:
+                prepare_do(i // per_chunk + 1)
+            if i + 2 < TILES:
+                multiply_values(i + 2)
+            if i >= 1:
+                finish(i - 1)
+        finish(TILES - 1)

@@ -19,7 +19,7 @@ ACT = mybir.ActivationFunctionType
 P = 128
 PACK = 4
 TILES = R // P
-Q_CHUNKS = (256, 256, 512)
+Q_CHUNK = 512
 DO_CHUNK = 256
 
 
@@ -31,7 +31,7 @@ def tile_attend_gat_lse_q_ts_kernel(tc, qT, kT, vT, doT, lse, delta, rw, ts, off
         psum = ctx.enter_context(tc.psum_pool(name="psum", bufs=1))
 
         def bank(tag, name):
-            return psum.tile([P, 512], F32, name=name, tag=tag, bufs={"A": 3, "B": 2, "C": 3}[tag])
+            return psum.tile([P, 512], F32, name=name, tag=tag, bufs={"A": 2, "B": 2, "C": 4}[tag])
 
         def quantize(src, width, fmt, name, pool=keep, tag=None):
             codes = pool.tile([P, width], U32, name=name + "_codes", tag=(tag or name) + "_codes", align_bytes=64)
@@ -39,29 +39,31 @@ def tile_attend_gat_lse_q_ts_kernel(tc, qT, kT, vT, doT, lse, delta, rw, ts, off
             nc.vector.quantize_mx(out=codes[:].bitcast(fmt), scales=scales[:], in_=src)
             return codes, scales
 
-        def interleave(engine, raw, width, name, tag):
-            grouped = keep.tile([P, width * PACK], BF16, name=name, tag=tag, align_bytes=64)
-            dst = grouped[:].rearrange("p (c i j) -> p c j i", i=4, j=PACK)
-            src = raw[:].rearrange("p j (c i) -> p c j i", i=4)
-            if engine == "vector":
-                nc.vector.tensor_copy(out=dst, in_=src)
-            else:
-                nc.scalar.copy(out=dst, in_=src)
+        def interleave(pieces, name, tag):
+            share = pieces[0][0].shape[2]
+            grouped = keep.tile([P, len(pieces) * share * PACK], BF16, name=name, tag=tag, align_bytes=64)
+            for n, (raw, engine) in enumerate(pieces):
+                dst = grouped[:, n * share * PACK : (n + 1) * share * PACK].rearrange("p (c i j) -> p c j i", i=4, j=PACK)
+                src = raw[:].rearrange("p j (c i) -> p c j i", i=4)
+                if engine == "vector":
+                    nc.vector.tensor_copy(out=dst, in_=src)
+                else:
+                    nc.scalar.copy(out=dst, in_=src)
             return grouped
 
         offsets = keep.tile([P, N // 16], U16, name="offsets")
         nc.sync.dma_start(offsets[:], offs)
 
         rows = keep.tile([P, P], F32, name="rows")
-        nc.gpsimd.memset(rows[:], 0.0)
+        nc.gpsimd.memset(rows[32:64, :], 0.0)
+        nc.gpsimd.memset(rows[64:128, :], 0.0)
         ts_pool = keep.tile([P, T], F32, name="ts_pool")
-        nc.vector.memset(ts_pool[32:64, :], 0.0)
-        nc.vector.memset(ts_pool[64:128, :], 0.0)
+        nc.vector.memset(ts_pool[:], 0.0)
         ident = keep.tile([P, P], F32, name="ident")
         make_identity(nc, ident[:])
-        nc.sync.dma_start(out=ts_pool[0:32, :], in_=ts[0:32, :])
-        for n, vec in enumerate((rw, lse, delta)):
-            nc.scalar.dma_start(out=rows[TILES * n : TILES * (n + 1), :], in_=vec[0].rearrange("(i m) o -> i (m o)", m=P))
+        for n, vec in enumerate((rw, rw, delta, lse)):
+            nc.sync.dma_start(out=rows[TILES * n : TILES * (n + 1), :], in_=vec[0].rearrange("(i m) o -> i (m o)", m=P))
+        nc.scalar.dma_start(out=ts_pool[0:1, :], in_=ts[0:1, :])
 
         q_view = qT[0].rearrange("(p j) r -> p j r", j=PACK)
         do_view = doT[0].rearrange("(p j) r -> p j r", j=PACK)
@@ -69,68 +71,62 @@ def tile_attend_gat_lse_q_ts_kernel(tc, qT, kT, vT, doT, lse, delta, rw, ts, off
         v_view = vT.rearrange("(p j) t -> p j t", j=PACK)
 
         def load(view, name, tag):
-            raw = keep.tile(list(view.shape), F32, name=name, tag=tag)
+            raw = keep.tile(list(view.shape), F32, name=name, tag=tag, align_bytes=64)
             nc.sync.dma_start(out=raw[:], in_=view)
             return raw
 
-        q_starts = [sum(Q_CHUNKS[:c]) for c in range(len(Q_CHUNKS))]
         k_pool = [load(k_view[:, j, :], "k_pool%d" % j, "plane%d" % j) for j in range(PACK)]
-        q_raw = [load(q_view[:, :, a : a + w], "q_raw%d" % a, "q_raw%d" % a) for a, w in zip(q_starts, Q_CHUNKS)]
+        q_first = load(q_view[:, :, 0 : Q_CHUNK // 2], "q_first", "q_first")
+        q_second = load(q_view[:, :, Q_CHUNK // 2 : Q_CHUNK], "q_second", "wide")
+        q_rest = load(q_view[:, :, Q_CHUNK:R], "q_rest", "q_rest")
 
         ts_row = keep.tile([P, N], F32, name="ts_row")
         nc.vector.tensor_copy(out=ts_row[:], in_=ts_pool[:].indirect(offsets[:]))
-        ts_by_block = bank("B", "ts_by_block")
         ts_by_place = bank("B", "ts_by_place")
         rows_t = bank("C", "rows_t")
-        for j in range(PACK):
-            nc.tensor.transpose(ts_by_block[:, j * P : (j + 1) * P], ts_row[:, j * P : (j + 1) * P], ident[:])
         for t in range(PACK):
             nc.tensor.transpose(ts_by_place[:, t * P : (t + 1) * P], ts_row[:, t:N:PACK], ident[:])
         nc.tensor.transpose(rows_t[:, 0:P], rows[:], ident[:])
+        absolute = keep.tile([P, 12], F32, name="absolute")
+        nc.scalar.activation(absolute[:, 0:8], rows_t[:, 0:8], ACT.Abs)
         cols = keep.tile([P, 32], F32, name="cols")
-        nc.scalar.copy(out=cols[:, 0:4], in_=ts_by_block[:, 0:N:P])
-        nc.scalar.copy(out=cols[:, 4:8], in_=ts_by_place[:, 0:N:P])
-        nc.scalar.copy(out=cols[:, 8:32], in_=rows_t[:, 0:24])
-        factors = cols[:, 0:16]
-        positive = keep.tile([P, 16], F32, name="positive")
-        nc.gpsimd.tensor_scalar(positive[:], factors, 0.0, 2.0, ALU.is_ge, ALU.mult)
-        sign = keep.tile([P, 16], F32, name="sign")
-        nc.gpsimd.tensor_scalar(sign[:], positive[:], -1.0, None, ALU.add)
-        absolute = keep.tile([P, 16], F32, name="absolute")
-        nc.gpsimd.tensor_tensor(absolute[:], factors, sign[:], ALU.mult)
-        size = keep.tile([P, 16], F32, name="size")
-        nc.gpsimd.tensor_scalar(size[:], absolute[:], 2.0**-126, None, ALU.max)
-        parts = keep.tile([P, 48], F32, name="parts", tag="first", align_bytes=64)
-        nc.gpsimd.tensor_scalar(parts[:, 0:16], size[:], 2.0**64, 2.0**-63, ALU.min, ALU.max)
-        nc.gpsimd.tensor_scalar(parts[:, 16:32], size[:], 2.0**-64, 1.0, ALU.mult, ALU.max)
-        nc.gpsimd.tensor_scalar(parts[:, 32:48], size[:], 2.0**63, 1.0, ALU.mult, ALU.min)
-        log_parts = keep.tile([P, 48], F32, name="log_parts", tag="second", align_bytes=64)
-        nc.scalar.activation(log_parts[:], parts[:], ACT.Ln)
-        log_edges = keep.tile([P, 16], F32, name="log_edges")
-        nc.gpsimd.tensor_tensor(log_edges[:], log_parts[:, 16:32], log_parts[:, 32:48], ALU.add)
-        log_size = keep.tile([P, 16], F32, name="log_size")
-        nc.gpsimd.tensor_tensor(log_size[:], log_parts[:, 0:16], log_edges[:], ALU.add)
-        exp_bias = keep.tile([P, TILES], F32, name="exp_bias")
-        nc.gpsimd.tensor_tensor(exp_bias[:], log_size[:, 8:16], cols[:, 16:24], ALU.subtract)
+        nc.scalar.copy(out=cols[:, 4:32], in_=rows_t[:, 8:36])
+        nc.scalar.activation(absolute[:, 8:12], ts_by_place[:, 0:N:P], ACT.Abs)
+        nc.scalar.copy(out=cols[:, 0:4], in_=ts_by_place[:, 0:N:P])
+        parts = keep.tile([P, 36], F32, name="parts")
+        nc.vector.tensor_scalar(parts[:, 0:12], absolute[:], 2.0**64, 2.0**-63, ALU.min, ALU.max)
+        nc.vector.tensor_scalar(parts[:, 12:24], absolute[:], 2.0**-64, 1.0, ALU.mult, ALU.max)
+        nc.vector.tensor_scalar(parts[:, 24:36], absolute[:], 2.0**-63, 2.0**-126, ALU.min, ALU.max)
+        positive = keep.tile([P, 12], F32, name="positive")
+        nc.vector.tensor_scalar(positive[:], cols[:, 0:12], 0.0, 2.0, ALU.is_ge, ALU.mult)
+        log_parts = keep.tile([P, 36], F32, name="log_parts")
+        nc.scalar.activation(log_parts[:, 0:24], parts[:, 0:24], ACT.Ln)
+        nc.scalar.activation(log_parts[:, 24:36], parts[:, 24:36], ACT.Ln, scale=2.0**63)
+        sign = keep.tile([P, 12], F32, name="sign")
+        nc.vector.tensor_scalar(sign[:], positive[:], -1.0, None, ALU.add)
+        log_upper = keep.tile([P, 12], F32, name="log_upper")
+        nc.vector.tensor_tensor(log_upper[:], log_parts[:, 0:12], log_parts[:, 12:24], ALU.add)
+        log_lower = keep.tile([P, 12], F32, name="log_lower")
+        nc.vector.tensor_tensor(log_lower[:], log_parts[:, 24:36], cols[:, 20:32], ALU.subtract)
+        shift = keep.tile([P, 12], F32, name="shift")
+        nc.vector.tensor_tensor(shift[:], log_upper[:], log_lower[:], ALU.add)
 
         k_bf = keep.tile([P, N * PACK], BF16, name="k_bf", align_bytes=64)
+        k_slots = k_bf[:].rearrange("p (t s j) -> p j s t", t=PACK, j=PACK)
         for j in range(PACK):
-            nc.vector.tensor_copy(out=k_bf[:, j : N * PACK : PACK], in_=k_pool[j][:].indirect(offsets[:]))
+            nc.vector.tensor_copy(out=k_slots[:, j], in_=k_pool[j][:].indirect(offsets[:]))
         k_codes, k_scales = quantize(k_bf[:], N, E4M3, "k")
 
         weights = []
 
-        def prepare_q(c, engine, tag):
-            return quantize(interleave(engine, q_raw[c], Q_CHUNKS[c], "q_bf%d" % c, tag)[:], Q_CHUNKS[c], E4M3, "q%d" % c)
-
-        def weigh(c, q_mx):
+        def weigh(half, q_mx):
             q_codes, q_scales = q_mx
-            width = Q_CHUNKS[c]
-            logits = []
+            per_half = Q_CHUNK // P
+            turned = [bank("C", "turned%d" % m) for m in range(per_half)]
             for j in range(PACK):
                 scores = bank("A", "scores")
                 nc.tensor.matmul_mx(
-                    out=scores[:, 0:width],
+                    out=scores[:],
                     lhsT=k_codes[:, j * P : (j + 1) * P].bitcast(E4M3),
                     lhsT_scale=k_scales[:, j * P : (j + 1) * P],
                     rhs=q_codes[:].bitcast(E4M3),
@@ -138,27 +134,22 @@ def tile_attend_gat_lse_q_ts_kernel(tc, qT, kT, vT, doT, lse, delta, rw, ts, off
                     start=True,
                     stop=True,
                 )
-                logit = keep.tile([P, width], F32, name="logit%d_%d" % (c, j), tag="logit%d_%d" % (c, j), align_bytes=64)
-                nc.scalar.activation(logit[:], scores[:, 0:width], ACT.Identity, bias=log_size[:, j : j + 1], scale=cols[:, j : j + 1])
-                logits.append(logit)
-            for m in range(width // P):
-                i = q_starts[c] // P + m
-                turned = bank("C", "turned")
-                for j in range(PACK):
-                    nc.tensor.transpose(turned[:, j * P : (j + 1) * P], logits[j][:, m * P : (m + 1) * P], ident[:])
+                logit = keep.tile([P, Q_CHUNK], F32, name="logit%d_%d" % (half, j), tag="logit%d_%d" % (half, j), align_bytes=64)
+                nc.scalar.activation(logit[:], scores[:], ACT.Identity, bias=shift[:, 8 + j : 9 + j], scale=cols[:, j : j + 1])
+                for m in range(per_half):
+                    nc.tensor.transpose(turned[m][:, j * P : (j + 1) * P], logit[:, m * P : (m + 1) * P], ident[:])
+            for m in range(per_half):
+                i = half * per_half + m
                 weight = keep.tile([P, N], F32, name="weight%d" % i, tag="weight%d" % i, align_bytes=64)
                 nc.scalar.activation(
                     weight[:].rearrange("p (u s e) -> p u s e", u=2, e=2),
-                    turned[:].rearrange("p (s u e) -> p u s e", u=2, e=2),
+                    turned[m][:].rearrange("p (u e s) -> p u s e", u=2, e=2),
                     ACT.Exp,
-                    bias=exp_bias[:, i : i + 1],
+                    bias=shift[:, i : i + 1],
                 )
                 weights.append(weight)
 
-        q_first = prepare_q(0, "scalar", "first")
-        q_second = prepare_q(1, "scalar", "second")
-        weigh(0, q_first)
-        weigh(1, q_second)
+        weigh(0, quantize(interleave([(q_first, "scalar"), (q_second, "vector")], "q_bf0", "plane3")[:], Q_CHUNK, E4M3, "q0"))
 
         k_words = k_bf[:].bitcast(F32)
         ks_bf = keep.tile([P, D * PACK], BF16, name="ks_bf", tag="wide", align_bytes=64)
@@ -166,31 +157,36 @@ def tile_attend_gat_lse_q_ts_kernel(tc, qT, kT, vT, doT, lse, delta, rw, ts, off
         for u in range(2):
             k_turned = bank("B", "k_turned")
             for t in range(PACK):
-                nc.tensor.transpose(k_turned[:, t * P : (t + 1) * P], k_words[:, 2 * t + u : 2 * N : 2 * PACK], ident[:])
+                nc.tensor.transpose(k_turned[:, t * P : (t + 1) * P], k_words[:, 2 * P * t + u : 2 * P * (t + 1) : 2], ident[:])
             nc.vector.tensor_tensor(
                 ks_view[:, u],
                 k_turned[:].bitcast(BF16).rearrange("s (t p e) -> s p e t", t=PACK, e=2),
-                sign[:, 4:8].unsqueeze(1).unsqueeze(1).to_broadcast([P, P, 2, PACK]),
+                sign[:, 0:4].unsqueeze(1).unsqueeze(1).to_broadcast([P, P, 2, PACK]),
                 ALU.mult,
             )
         ks_codes, ks_scales = quantize(ks_bf[:], D, E4M3, "ks")
-        weigh(2, prepare_q(2, "vector", "wide"))
+        weigh(1, quantize(interleave([(q_rest, "vector")], "q_bf1", "wide")[:], Q_CHUNK, E4M3, "q1"))
 
         v_pool = [load(v_view[:, j, :], "v_pool%d" % j, "plane%d" % j) for j in range(PACK)]
         v_bf = keep.tile([P, N * PACK], BF16, name="v_bf", tag="wide", align_bytes=64)
         v_view_bf = v_bf[:].rearrange("p (u s e j) -> p j s u e", u=2, e=2, j=PACK)
         for j in range(PACK):
             nc.vector.tensor_copy(out=v_view_bf[:, j], in_=v_pool[j][:].indirect(offsets[:]))
-        v_codes, v_scales = quantize(v_bf[:], N, E4M3, "v")
 
-        do_raw = [load(do_view[:, :, c * DO_CHUNK : (c + 1) * DO_CHUNK], "do_raw%d" % c, "plane%d" % c) for c in range(R // DO_CHUNK)]
-        do_tags = ("logit2_3", "wide", "weight0", "weight2")
+        do_tags = ("plane3", "logit1_3", "weight0", "weight2")
         do_mx = {}
         per_chunk = DO_CHUNK // P
 
+        def cast_do(c):
+            raw = load(do_view[:, :, c * DO_CHUNK : (c + 1) * DO_CHUNK], "do_raw%d" % c, "plane%d" % c)
+            return interleave([(raw, "vector" if c % 2 == 0 else "scalar")], "do_bf%d" % c, do_tags[c])
+
         def prepare_do(c):
-            grouped = interleave("scalar" if c % 2 == 0 else "vector", do_raw[c], DO_CHUNK, "do_bf%d" % c, do_tags[c])
-            do_mx[c] = quantize(grouped[:], DO_CHUNK, E5M2, "do%d" % c)
+            do_mx[c] = quantize(cast_do(c)[:], DO_CHUNK, E5M2, "do%d" % c)
+
+        do_first = cast_do(0)
+        v_codes, v_scales = quantize(v_bf[:], N, E4M3, "v")
+        do_mx[0] = quantize(do_first[:], DO_CHUNK, E5M2, "do0")
 
         dp, ds_t, ds_mx = {}, {}, {}
 
@@ -210,7 +206,7 @@ def tile_attend_gat_lse_q_ts_kernel(tc, qT, kT, vT, doT, lse, delta, rw, ts, off
 
         def make_ds(i):
             ds = ring.tile([P, N], BF16, name="ds", align_bytes=64)
-            nc.vector.scalar_tensor_tensor(ds[:], dp[i][:], cols[:, 24 + i : 25 + i], weights[i][:], ALU.subtract, ALU.mult)
+            nc.vector.scalar_tensor_tensor(ds[:], dp[i][:], cols[:, 12 + i : 13 + i], weights[i][:], ALU.subtract, ALU.mult)
             ds_words = ds[:].bitcast(F32)
             ds_turned = bank("B", "ds_turned")
             for u in range(2):
@@ -234,10 +230,9 @@ def tile_attend_gat_lse_q_ts_kernel(tc, qT, kT, vT, doT, lse, delta, rw, ts, off
                 stop=True,
             )
             result = ring.tile([P, D], F32, name="result")
-            nc.scalar.activation(result[:], grad[:], ACT.Copy, scale=sign[:, 8 + i : 9 + i])
+            nc.scalar.activation(result[:], grad[:], ACT.Copy, scale=sign[:, 4 + i : 5 + i])
             nc.sync.dma_start(out=out[0, i * P : (i + 1) * P, :], in_=result[:])
 
-        prepare_do(0)
         multiply_values(0)
         multiply_values(1)
         for i in range(TILES):

@@ -52,19 +52,6 @@ def tile_attend_gat_lse_q_ts_kernel(tc, qT, kT, vT, doT, lse, delta, rw, ts, off
             return grouped
 
         offsets = keep.tile([P, N // 16], U16, name="offsets")
-        nc.sync.dma_start(offsets[:], offs)
-
-        rows = keep.tile([P, P], F32, name="rows")
-        nc.gpsimd.memset(rows[32:64, :], 0.0)
-        nc.gpsimd.memset(rows[64:128, :], 0.0)
-        ts_pool = keep.tile([P, T], F32, name="ts_pool")
-        nc.vector.memset(ts_pool[:], 0.0)
-        ident = keep.tile([P, P], F32, name="ident")
-        make_identity(nc, ident[:])
-        for n, vec in enumerate((rw, rw, delta, lse)):
-            nc.sync.dma_start(out=rows[TILES * n : TILES * (n + 1), :], in_=vec[0].rearrange("(i m) o -> i (m o)", m=P))
-        nc.scalar.dma_start(out=ts_pool[0:1, :], in_=ts[0:1, :])
-
         q_view = qT[0].rearrange("(p j) r -> p j r", j=PACK)
         do_view = doT[0].rearrange("(p j) r -> p j r", j=PACK)
         k_view = kT.rearrange("(p j) t -> p j t", j=PACK)
@@ -75,9 +62,24 @@ def tile_attend_gat_lse_q_ts_kernel(tc, qT, kT, vT, doT, lse, delta, rw, ts, off
             nc.sync.dma_start(out=raw[:], in_=view)
             return raw
 
-        k_pool = [load(k_view[:, j, :], "k_pool%d" % j, "plane%d" % j) for j in range(PACK)]
+        k_pool = [load(k_view[:, 0, :], "k_pool0", "plane0")]
+        nc.sync.dma_start(offsets[:], offs)
+
+        rows = keep.tile([P, P], F32, name="rows")
+        nc.gpsimd.memset(rows[32:64, :], 0.0)
+        nc.gpsimd.memset(rows[64:128, :], 0.0)
+        ts_pool = keep.tile([P, T], F32, name="ts_pool")
+        nc.vector.memset(ts_pool[32:64, :], 0.0)
+        nc.gpsimd.memset(ts_pool[64:128, :], 0.0)
+        ident = keep.tile([P, P], F32, name="ident")
+        make_identity(nc, ident[:])
+        for n, vec in enumerate((rw, rw, delta, lse)):
+            nc.sync.dma_start(out=rows[TILES * n : TILES * (n + 1), :], in_=vec[0].rearrange("(i m) o -> i (m o)", m=P))
+        nc.sync.dma_start(out=ts_pool[0:32, :], in_=ts[0:32, :])
+
+        k_pool.extend(load(k_view[:, j, :], "k_pool%d" % j, "plane%d" % j) for j in range(1, PACK))
         q_first = load(q_view[:, :, 0 : Q_CHUNK // 2], "q_first", "q_first")
-        q_second = load(q_view[:, :, Q_CHUNK // 2 : Q_CHUNK], "q_second", "wide")
+        q_second = load(q_view[:, :, Q_CHUNK // 2 : Q_CHUNK], "q_second", "q_second")
         q_rest = load(q_view[:, :, Q_CHUNK:R], "q_rest", "q_rest")
 
         ts_row = keep.tile([P, N], F32, name="ts_row")
@@ -102,6 +104,8 @@ def tile_attend_gat_lse_q_ts_kernel(tc, qT, kT, vT, doT, lse, delta, rw, ts, off
         log_parts = keep.tile([P, 36], F32, name="log_parts")
         nc.scalar.activation(log_parts[:, 0:24], parts[:, 0:24], ACT.Ln)
         nc.scalar.activation(log_parts[:, 24:36], parts[:, 24:36], ACT.Ln, scale=2.0**63)
+        warm = keep.tile([P, 1], F32, name="warm")
+        nc.scalar.activation(warm[:], log_parts[:, 24:25], ACT.Exp)
         sign = keep.tile([P, 12], F32, name="sign")
         nc.vector.tensor_scalar(sign[:], positive[:], -1.0, None, ALU.add)
         log_upper = keep.tile([P, 12], F32, name="log_upper")
@@ -112,9 +116,13 @@ def tile_attend_gat_lse_q_ts_kernel(tc, qT, kT, vT, doT, lse, delta, rw, ts, off
         nc.vector.tensor_tensor(shift[:], log_upper[:], log_lower[:], ALU.add)
 
         k_bf = keep.tile([P, N * PACK], BF16, name="k_bf", align_bytes=64)
-        k_slots = k_bf[:].rearrange("p (t s j) -> p j s t", t=PACK, j=PACK)
+        k_picked = keep.tile([P, PACK, N], F32, name="k_picked", tag="picked", align_bytes=64)
         for j in range(PACK):
-            nc.vector.tensor_copy(out=k_slots[:, j], in_=k_pool[j][:].indirect(offsets[:]))
+            nc.vector.tensor_copy(out=k_picked[:, j, :], in_=k_pool[j][:].indirect(offsets[:]))
+        nc.vector.tensor_copy(
+            out=k_bf[:].rearrange("p (t s j) -> p s j t", t=PACK, j=PACK),
+            in_=k_picked[:].rearrange("p j (s t) -> p s j t", t=PACK),
+        )
         k_codes, k_scales = quantize(k_bf[:], N, E4M3, "k")
 
         weights = []
@@ -124,7 +132,7 @@ def tile_attend_gat_lse_q_ts_kernel(tc, qT, kT, vT, doT, lse, delta, rw, ts, off
             per_half = Q_CHUNK // P
             turned = [bank("C", "turned%d" % m) for m in range(per_half)]
             for j in range(PACK):
-                scores = bank("A", "scores")
+                scores = bank("A" if j < 2 else "B", "scores")
                 nc.tensor.matmul_mx(
                     out=scores[:],
                     lhsT=k_codes[:, j * P : (j + 1) * P].bitcast(E4M3),
@@ -149,13 +157,13 @@ def tile_attend_gat_lse_q_ts_kernel(tc, qT, kT, vT, doT, lse, delta, rw, ts, off
                 )
                 weights.append(weight)
 
-        weigh(0, quantize(interleave([(q_first, "scalar"), (q_second, "vector")], "q_bf0", "plane3")[:], Q_CHUNK, E4M3, "q0"))
+        q_mx = quantize(interleave([(q_first, "scalar"), (q_second, "scalar")], "q_bf0", "plane2")[:], Q_CHUNK, E4M3, "q0")
 
         k_words = k_bf[:].bitcast(F32)
         ks_bf = keep.tile([P, D * PACK], BF16, name="ks_bf", tag="wide", align_bytes=64)
         ks_view = ks_bf[:].rearrange("s (p u e t) -> s u p e t", u=2, e=2, t=PACK)
         for u in range(2):
-            k_turned = bank("B", "k_turned")
+            k_turned = bank("C", "k_turned")
             for t in range(PACK):
                 nc.tensor.transpose(k_turned[:, t * P : (t + 1) * P], k_words[:, 2 * P * t + u : 2 * P * (t + 1) : 2], ident[:])
             nc.vector.tensor_tensor(
@@ -164,22 +172,27 @@ def tile_attend_gat_lse_q_ts_kernel(tc, qT, kT, vT, doT, lse, delta, rw, ts, off
                 sign[:, 0:4].unsqueeze(1).unsqueeze(1).to_broadcast([P, P, 2, PACK]),
                 ALU.mult,
             )
+        weigh(0, q_mx)
         ks_codes, ks_scales = quantize(ks_bf[:], D, E4M3, "ks")
         weigh(1, quantize(interleave([(q_rest, "vector")], "q_bf1", "wide")[:], Q_CHUNK, E4M3, "q1"))
 
-        v_pool = [load(v_view[:, j, :], "v_pool%d" % j, "plane%d" % j) for j in range(PACK)]
-        v_bf = keep.tile([P, N * PACK], BF16, name="v_bf", tag="wide", align_bytes=64)
-        v_view_bf = v_bf[:].rearrange("p (u s e j) -> p j s u e", u=2, e=2, j=PACK)
+        v_pool = [load(v_view[:, j, :], "v_pool%d" % j, "plane%d" % (0, 1, 3, 2)[j]) for j in range(PACK)]
+        v_picked = keep.tile([P, PACK, N], F32, name="v_picked", tag="wide", align_bytes=64)
         for j in range(PACK):
-            nc.vector.tensor_copy(out=v_view_bf[:, j], in_=v_pool[j][:].indirect(offsets[:]))
+            nc.vector.tensor_copy(out=v_picked[:, j, :], in_=v_pool[j][:].indirect(offsets[:]))
+        v_bf = keep.tile([P, N * PACK], BF16, name="v_bf", tag="picked", align_bytes=64)
+        nc.vector.tensor_copy(
+            out=v_bf[:].rearrange("p (u s e j) -> p s j u e", u=2, e=2, j=PACK),
+            in_=v_picked[:].rearrange("p j (s u e) -> p s j u e", u=2, e=2),
+        )
 
-        do_tags = ("plane3", "logit1_3", "weight0", "weight2")
+        do_tags = ("plane2", "picked", "weight0", "weight2")
         do_mx = {}
         per_chunk = DO_CHUNK // P
 
         def cast_do(c):
-            raw = load(do_view[:, :, c * DO_CHUNK : (c + 1) * DO_CHUNK], "do_raw%d" % c, "plane%d" % c)
-            return interleave([(raw, "vector" if c % 2 == 0 else "scalar")], "do_bf%d" % c, do_tags[c])
+            raw = load(do_view[:, :, c * DO_CHUNK : (c + 1) * DO_CHUNK], "do_raw%d" % c, "plane%d" % (0, 1, 3, 2)[c])
+            return interleave([(raw, "vector" if c < 3 else "scalar")], "do_bf%d" % c, do_tags[c])
 
         def prepare_do(c):
             do_mx[c] = quantize(cast_do(c)[:], DO_CHUNK, E5M2, "do%d" % c)
@@ -193,7 +206,7 @@ def tile_attend_gat_lse_q_ts_kernel(tc, qT, kT, vT, doT, lse, delta, rw, ts, off
         def multiply_values(i):
             codes, scales = do_mx[i // per_chunk]
             cols_i = slice((i % per_chunk) * P, (i % per_chunk + 1) * P)
-            dp[i] = bank("A", "dp")
+            dp[i] = bank("C" if i % 3 == 2 else "A", "dp")
             nc.tensor.matmul_mx(
                 out=dp[i][:],
                 lhsT=codes[:, cols_i].bitcast(E5M2),
@@ -235,12 +248,14 @@ def tile_attend_gat_lse_q_ts_kernel(tc, qT, kT, vT, doT, lse, delta, rw, ts, off
 
         multiply_values(0)
         multiply_values(1)
+        prepare_do(1)
+        multiply_values(2)
         for i in range(TILES):
             make_ds(i)
-            if i % per_chunk == 0 and i // per_chunk + 1 < R // DO_CHUNK:
-                prepare_do(i // per_chunk + 1)
-            if i + 2 < TILES:
-                multiply_values(i + 2)
+            if i in (0, 2):
+                prepare_do(i // per_chunk + 2)
+            if i + 3 < TILES:
+                multiply_values(i + 3)
             if i >= 1:
                 finish(i - 1)
         finish(TILES - 1)

@@ -30,8 +30,8 @@ def tile_attend_gat_lse_q_ts_kernel(tc, qT, kT, vT, doT, lse, delta, rw, ts, off
         ring = ctx.enter_context(tc.tile_pool(name="ring", bufs=4))
         psum = ctx.enter_context(tc.psum_pool(name="psum", bufs=1))
 
-        def bank(tag, name):
-            return psum.tile([P, 512], F32, name=name, tag=tag, bufs={"A": 2, "B": 2, "C": 4}[tag])
+        def bank(number, name):
+            return psum.tile([P, 512], F32, name=name, tag="bank%d" % number)
 
         def quantize(src, width, fmt, name, pool=keep, tag=None):
             codes = pool.tile([P, width], U32, name=name + "_codes", tag=(tag or name) + "_codes", align_bytes=64)
@@ -39,12 +39,13 @@ def tile_attend_gat_lse_q_ts_kernel(tc, qT, kT, vT, doT, lse, delta, rw, ts, off
             nc.vector.quantize_mx(out=codes[:].bitcast(fmt), scales=scales[:], in_=src)
             return codes, scales
 
-        def interleave(pieces, name, tag):
-            share = pieces[0][0].shape[2]
-            grouped = keep.tile([P, len(pieces) * share * PACK], BF16, name=name, tag=tag, align_bytes=64)
-            for n, (raw, engine) in enumerate(pieces):
+        def interleave(raw, engines, name, tag):
+            width = raw.shape[2]
+            share = width // len(engines)
+            grouped = keep.tile([P, width * PACK], BF16, name=name, tag=tag, align_bytes=64)
+            for n, engine in enumerate(engines):
                 dst = grouped[:, n * share * PACK : (n + 1) * share * PACK].rearrange("p (c i j) -> p c j i", i=4, j=PACK)
-                src = raw[:].rearrange("p j (c i) -> p c j i", i=4)
+                src = raw[:, :, n * share : (n + 1) * share].rearrange("p j (c i) -> p c j i", i=4)
                 if engine == "vector":
                     nc.vector.tensor_copy(out=dst, in_=src)
                 else:
@@ -57,82 +58,110 @@ def tile_attend_gat_lse_q_ts_kernel(tc, qT, kT, vT, doT, lse, delta, rw, ts, off
         k_view = kT.rearrange("(p j) t -> p j t", j=PACK)
         v_view = vT.rearrange("(p j) t -> p j t", j=PACK)
 
-        def load(view, name, tag):
-            raw = keep.tile(list(view.shape), F32, name=name, tag=tag, align_bytes=64)
+        def load(view, name):
+            raw = keep.tile(list(view.shape), F32, name=name, tag=name, align_bytes=64)
             nc.sync.dma_start(out=raw[:], in_=view)
             return raw
 
-        k_pool = [load(k_view[:, 0, :], "k_pool0", "plane0")]
-        nc.sync.dma_start(offsets[:], offs)
-
         rows = keep.tile([P, P], F32, name="rows")
-        nc.gpsimd.memset(rows[32:64, :], 0.0)
-        nc.gpsimd.memset(rows[64:128, :], 0.0)
+        nc.vector.memset(rows[:], 0.0)
         ts_pool = keep.tile([P, T], F32, name="ts_pool")
-        nc.vector.memset(ts_pool[32:64, :], 0.0)
-        nc.gpsimd.memset(ts_pool[64:128, :], 0.0)
+        nc.vector.memset(ts_pool[:], 0.0)
         ident = keep.tile([P, P], F32, name="ident")
         make_identity(nc, ident[:])
-        for n, vec in enumerate((rw, rw, delta, lse)):
-            nc.sync.dma_start(out=rows[TILES * n : TILES * (n + 1), :], in_=vec[0].rearrange("(i m) o -> i (m o)", m=P))
-        nc.sync.dma_start(out=ts_pool[0:32, :], in_=ts[0:32, :])
+        warm_ln = keep.tile([P, 1], F32, name="warm_ln")
+        nc.scalar.activation(warm_ln[:], ident[:, 0:1], ACT.Ln, bias=1.0)
 
-        k_pool.extend(load(k_view[:, j, :], "k_pool%d" % j, "plane%d" % j) for j in range(1, PACK))
-        q_first = load(q_view[:, :, 0 : Q_CHUNK // 2], "q_first", "q_first")
-        q_second = load(q_view[:, :, Q_CHUNK // 2 : Q_CHUNK], "q_second", "q_second")
-        q_rest = load(q_view[:, :, Q_CHUNK:R], "q_rest", "q_rest")
+        k_pool = [load(k_view[:, 0, :], "k_pool0")]
+        nc.sync.dma_start(offsets[:], offs)
+        for n, vec in enumerate((rw, delta, lse)):
+            nc.sync.dma_start(out=rows[TILES * n : TILES * (n + 1), :], in_=vec[0].rearrange("(i m) o -> i (m o)", m=P))
+        nc.sync.dma_start(out=ts_pool[0:1, :], in_=ts[0:1, :])
+        k_pool.extend(load(k_view[:, j, :], "k_pool%d" % j) for j in range(1, PACK))
+        q_raw = [load(q_view[:, :, c * Q_CHUNK : (c + 1) * Q_CHUNK], "q_raw%d" % c) for c in range(R // Q_CHUNK)]
+        v_pool = [load(v_view[:, j, :], "v_pool%d" % j) for j in range(PACK)]
+        do_raw = [load(do_view[:, :, c * DO_CHUNK : (c + 1) * DO_CHUNK], "do_raw%d" % c) for c in range(R // DO_CHUNK)]
+
+        k_pairs = [keep.tile([P, 2 * N], BF16, name="k_pair%d" % a, align_bytes=64) for a in range(2)]
+
+        def gather_keys(j):
+            nc.vector.tensor_copy(out=k_pairs[j // 2][:, j % 2 * N : (j % 2 + 1) * N], in_=k_pool[j][:].indirect(offsets[:]))
+
+        gather_keys(0)
 
         ts_row = keep.tile([P, N], F32, name="ts_row")
         nc.vector.tensor_copy(out=ts_row[:], in_=ts_pool[:].indirect(offsets[:]))
-        ts_by_place = bank("B", "ts_by_place")
-        rows_t = bank("C", "rows_t")
+        ts_by_place = bank(0, "ts_by_place")
+        rows_t = bank(1, "rows_t")
+        nc.tensor.transpose(rows_t[:, 0:P], rows[:], ident[:])
         for t in range(PACK):
             nc.tensor.transpose(ts_by_place[:, t * P : (t + 1) * P], ts_row[:, t:N:PACK], ident[:])
-        nc.tensor.transpose(rows_t[:, 0:P], rows[:], ident[:])
+        ts_cols = ts_by_place[:, 0:N:P]
         absolute = keep.tile([P, 12], F32, name="absolute")
         nc.scalar.activation(absolute[:, 0:8], rows_t[:, 0:8], ACT.Abs)
-        cols = keep.tile([P, 32], F32, name="cols")
-        nc.scalar.copy(out=cols[:, 4:32], in_=rows_t[:, 8:36])
-        nc.scalar.activation(absolute[:, 8:12], ts_by_place[:, 0:N:P], ACT.Abs)
-        nc.scalar.copy(out=cols[:, 0:4], in_=ts_by_place[:, 0:N:P])
-        parts = keep.tile([P, 36], F32, name="parts")
-        nc.vector.tensor_scalar(parts[:, 0:12], absolute[:], 2.0**64, 2.0**-63, ALU.min, ALU.max)
-        nc.vector.tensor_scalar(parts[:, 12:24], absolute[:], 2.0**-64, 1.0, ALU.mult, ALU.max)
-        nc.vector.tensor_scalar(parts[:, 24:36], absolute[:], 2.0**-63, 2.0**-126, ALU.min, ALU.max)
-        positive = keep.tile([P, 12], F32, name="positive")
-        nc.vector.tensor_scalar(positive[:], cols[:, 0:12], 0.0, 2.0, ALU.is_ge, ALU.mult)
-        log_parts = keep.tile([P, 36], F32, name="log_parts")
-        nc.scalar.activation(log_parts[:, 0:24], parts[:, 0:24], ACT.Ln)
-        nc.scalar.activation(log_parts[:, 24:36], parts[:, 24:36], ACT.Ln, scale=2.0**63)
+        rw_sign = keep.tile([P, TILES], F32, name="rw_sign")
+        nc.scalar.activation(rw_sign[:], rows_t[:, 0:8], ACT.Sign)
+        cols = keep.tile([P, 12], F32, name="cols")
+        nc.scalar.copy(out=cols[:, 4:12], in_=rows_t[:, 8:16])
+        terms = keep.tile([P, 4, 12], F32, name="terms", tag="terms", align_bytes=64)
+        nc.scalar.activation(terms[:, 3, :], rows_t[:, 16:28], ACT.Copy, scale=-1.0)
+        nc.scalar.activation(absolute[:, 8:12], ts_cols, ACT.Abs)
+        nc.scalar.copy(out=cols[:, 0:4], in_=ts_cols)
+        ts_sign = keep.tile([P, 2, PACK], BF16, name="ts_sign")
+        nc.scalar.activation(ts_sign[:], ts_cols.unsqueeze(1).to_broadcast([P, 2, PACK]), ACT.Sign)
+        parts = keep.tile([P, 3, 12], F32, name="parts")
+        nc.gpsimd.tensor_scalar(parts[:, 0, :], absolute[:], 2.0**64, 2.0**-63, ALU.min, ALU.max)
+        nc.gpsimd.tensor_scalar(parts[:, 1, :], absolute[:], 2.0**-64, 1.0, ALU.mult, ALU.max)
+        nc.gpsimd.tensor_scalar(parts[:, 2, :], absolute[:], 2.0**-63, 2.0**-126, ALU.min, ALU.max)
+        nc.scalar.activation(terms[:, 0:2, :], parts[:, 0:2, :], ACT.Ln)
+        nc.scalar.activation(terms[:, 2, :], parts[:, 2, :], ACT.Ln, scale=2.0**63)
         warm = keep.tile([P, 1], F32, name="warm")
-        nc.scalar.activation(warm[:], log_parts[:, 24:25], ACT.Exp)
-        sign = keep.tile([P, 12], F32, name="sign")
-        nc.vector.tensor_scalar(sign[:], positive[:], -1.0, None, ALU.add)
-        log_upper = keep.tile([P, 12], F32, name="log_upper")
-        nc.vector.tensor_tensor(log_upper[:], log_parts[:, 0:12], log_parts[:, 12:24], ALU.add)
-        log_lower = keep.tile([P, 12], F32, name="log_lower")
-        nc.vector.tensor_tensor(log_lower[:], log_parts[:, 24:36], cols[:, 20:32], ALU.subtract)
-        shift = keep.tile([P, 12], F32, name="shift")
-        nc.vector.tensor_tensor(shift[:], log_upper[:], log_lower[:], ALU.add)
+        nc.scalar.activation(warm[:], terms[:, 2, 0:1], ACT.Exp)
 
-        k_bf = keep.tile([P, N * PACK], BF16, name="k_bf", align_bytes=64)
-        k_picked = keep.tile([P, PACK, N], F32, name="k_picked", tag="picked", align_bytes=64)
-        for j in range(PACK):
-            nc.vector.tensor_copy(out=k_picked[:, j, :], in_=k_pool[j][:].indirect(offsets[:]))
-        nc.vector.tensor_copy(
-            out=k_bf[:].rearrange("p (t s j) -> p s j t", t=PACK, j=PACK),
-            in_=k_picked[:].rearrange("p j (s t) -> p s j t", t=PACK),
-        )
+        def turn_keys(a, number):
+            words = k_pairs[a][:].bitcast(F32)
+            turned = bank(number, "k_turned")
+            for w in range(4):
+                first = 2 * P * (w // 2)
+                nc.tensor.transpose(turned[:, w * P : (w + 1) * P], words[:, first + w % 2 : first + 2 * P : 2], ident[:])
+            return turned
+
+        def sign_keys(a, turned):
+            nc.vector.tensor_tensor(
+                ks_bf[:].rearrange("s (p a w e) -> s a p w e", a=2, w=4, e=2)[:, a],
+                turned[:].bitcast(BF16).rearrange("s (w p e) -> s p w e", w=4, e=2),
+                ts_sign[:].rearrange("s j (u e) -> s (j u) e", e=2).unsqueeze(1).to_broadcast([P, P, 4, 2]),
+                ALU.mult,
+            )
+
+        k_bf = keep.tile([P, N * PACK], BF16, name="k_bf", tag="k_bf", align_bytes=64)
+
+        def interleave_keys(a):
+            nc.vector.tensor_copy(
+                out=k_bf[:].rearrange("p (t s j) -> p s j t", t=PACK, j=PACK)[:, :, 2 * a : 2 * a + 2, :],
+                in_=k_pairs[a][:].rearrange("p (j s t) -> p s j t", j=2, t=PACK),
+            )
+
+        last = PACK - 1
+        gather_keys(1)
+        k_turned = turn_keys(0, 6)
+        interleave_keys(0)
+        gather_keys(2)
+        ks_bf = keep.tile([P, D * PACK], BF16, name="ks_bf", tag="k_pool2", align_bytes=64)
+        sign_keys(0, k_turned)
+        gather_keys(3)
+        shift = keep.tile([P, 12], F32, name="shift", tag="k_pool3", align_bytes=64)
+        nc.vector.tensor_reduce(shift[:], terms[:].rearrange("p g c -> p c g"), mybir.AxisListType.X, ALU.add)
+        interleave_keys(1)
         k_codes, k_scales = quantize(k_bf[:], N, E4M3, "k")
 
-        weights = []
+        per_half = Q_CHUNK // P
+        logits, weights = {}, []
 
-        def weigh(half, q_mx):
+        def score(half, q_mx):
             q_codes, q_scales = q_mx
-            per_half = Q_CHUNK // P
-            turned = [bank("C", "turned%d" % m) for m in range(per_half)]
             for j in range(PACK):
-                scores = bank("A" if j < 2 else "B", "scores")
+                scores = bank((j + half) % PACK, "scores")
                 nc.tensor.matmul_mx(
                     out=scores[:],
                     lhsT=k_codes[:, j * P : (j + 1) * P].bitcast(E4M3),
@@ -142,13 +171,21 @@ def tile_attend_gat_lse_q_ts_kernel(tc, qT, kT, vT, doT, lse, delta, rw, ts, off
                     start=True,
                     stop=True,
                 )
-                logit = keep.tile([P, Q_CHUNK], F32, name="logit%d_%d" % (half, j), tag="logit%d_%d" % (half, j), align_bytes=64)
+                logit = keep.tile([P, Q_CHUNK], F32, name="logit%d_%d" % (half, j), align_bytes=64)
                 nc.scalar.activation(logit[:], scores[:], ACT.Identity, bias=shift[:, 8 + j : 9 + j], scale=cols[:, j : j + 1])
+                logits[half, j] = logit
+
+        def turn_logits(half):
+            turned = [bank(4 + m, "turned%d" % m) for m in range(per_half)]
+            for j in range(PACK):
                 for m in range(per_half):
-                    nc.tensor.transpose(turned[m][:, j * P : (j + 1) * P], logit[:, m * P : (m + 1) * P], ident[:])
+                    nc.tensor.transpose(turned[m][:, j * P : (j + 1) * P], logits[half, j][:, m * P : (m + 1) * P], ident[:])
+            return turned
+
+        def weigh(half, turned):
             for m in range(per_half):
                 i = half * per_half + m
-                weight = keep.tile([P, N], F32, name="weight%d" % i, tag="weight%d" % i, align_bytes=64)
+                weight = keep.tile([P, N], F32, name="weight%d" % i, align_bytes=64)
                 nc.scalar.activation(
                     weight[:].rearrange("p (u s e) -> p u s e", u=2, e=2),
                     turned[m][:].rearrange("p (u e s) -> p u s e", u=2, e=2),
@@ -157,60 +194,63 @@ def tile_attend_gat_lse_q_ts_kernel(tc, qT, kT, vT, doT, lse, delta, rw, ts, off
                 )
                 weights.append(weight)
 
-        q_mx = quantize(interleave([(q_first, "scalar"), (q_second, "scalar")], "q_bf0", "plane2")[:], Q_CHUNK, E4M3, "q0")
-
-        k_words = k_bf[:].bitcast(F32)
-        ks_bf = keep.tile([P, D * PACK], BF16, name="ks_bf", tag="wide", align_bytes=64)
-        ks_view = ks_bf[:].rearrange("s (p u e t) -> s u p e t", u=2, e=2, t=PACK)
-        for u in range(2):
-            k_turned = bank("C", "k_turned")
-            for t in range(PACK):
-                nc.tensor.transpose(k_turned[:, t * P : (t + 1) * P], k_words[:, 2 * P * t + u : 2 * P * (t + 1) : 2], ident[:])
-            nc.vector.tensor_tensor(
-                ks_view[:, u],
-                k_turned[:].bitcast(BF16).rearrange("s (t p e) -> s p e t", t=PACK, e=2),
-                sign[:, 0:4].unsqueeze(1).unsqueeze(1).to_broadcast([P, P, 2, PACK]),
-                ALU.mult,
-            )
-        weigh(0, q_mx)
-        ks_codes, ks_scales = quantize(ks_bf[:], D, E4M3, "ks")
-        weigh(1, quantize(interleave([(q_rest, "vector")], "q_bf1", "wide")[:], Q_CHUNK, E4M3, "q1"))
-
-        v_pool = [load(v_view[:, j, :], "v_pool%d" % j, "plane%d" % (0, 1, 3, 2)[j]) for j in range(PACK)]
-        v_picked = keep.tile([P, PACK, N], F32, name="v_picked", tag="wide", align_bytes=64)
-        for j in range(PACK):
-            nc.vector.tensor_copy(out=v_picked[:, j, :], in_=v_pool[j][:].indirect(offsets[:]))
-        v_bf = keep.tile([P, N * PACK], BF16, name="v_bf", tag="picked", align_bytes=64)
-        nc.vector.tensor_copy(
-            out=v_bf[:].rearrange("p (u s e j) -> p s j u e", u=2, e=2, j=PACK),
-            in_=v_picked[:].rearrange("p j (s u e) -> p s j u e", u=2, e=2),
+        quarter = Q_CHUNK // 2
+        q_first = (
+            keep.tile([P, Q_CHUNK], U32, name="q0_codes", align_bytes=64),
+            keep.tile([P, Q_CHUNK], U8, name="q0_scales", align_bytes=64),
         )
+        for n, (engine, tag) in enumerate((("vector", "stage"), ("scalar", "terms"))):
+            part = slice(n * quarter, (n + 1) * quarter)
+            grouped = interleave(q_raw[0][:, :, part], (engine,), "q_bf0_%d" % n, tag)
+            nc.vector.quantize_mx(out=q_first[0][:, part].bitcast(E4M3), scales=q_first[1][:, part], in_=grouped[:])
+        score(0, q_first)
+        q_second = quantize(interleave(q_raw[1], ("vector",), "q_bf1", "stage")[:], Q_CHUNK, E4M3, "q1")
+        sign_keys(1, turn_keys(1, 0))
+        turned_first = turn_logits(0)
+        score(1, q_second)
+        weigh(0, turned_first)
+        weigh(1, turn_logits(1))
+        ks_codes, ks_scales = quantize(ks_bf[:], D, E4M3, "ks")
 
-        do_tags = ("plane2", "picked", "weight0", "weight2")
+        v_picked = keep.tile([P, last * N], BF16, name="v_picked", tag="stage", align_bytes=64)
+        for j in range(last):
+            nc.vector.tensor_copy(out=v_picked[:, j * N : (j + 1) * N], in_=v_pool[j][:].indirect(offsets[:]))
+        v_bf = keep.tile([P, N * PACK], BF16, name="v_bf", tag="v_bf", align_bytes=64)
+        v_places = v_bf[:].rearrange("p (u s e j) -> p s j u e", u=2, e=2, j=PACK)
+        nc.vector.tensor_copy(
+            out=v_places[:, :, 0:last],
+            in_=v_picked[:].rearrange("p (j s u e) -> p s j u e", j=last, u=2, e=2),
+        )
+        nc.vector.tensor_copy(out=v_places[:, :, last], in_=v_pool[last][:].indirect(offsets[:]))
+
         do_mx = {}
         per_chunk = DO_CHUNK // P
-
-        def cast_do(c):
-            raw = load(do_view[:, :, c * DO_CHUNK : (c + 1) * DO_CHUNK], "do_raw%d" % c, "plane%d" % (0, 1, 3, 2)[c])
-            return interleave([(raw, "vector" if c < 3 else "scalar")], "do_bf%d" % c, do_tags[c])
+        do_plan = (None, ("scalar", "k_pool3"), ("scalar", "do_raw1"), ("vector", "do_raw2"))
 
         def prepare_do(c):
-            do_mx[c] = quantize(cast_do(c)[:], DO_CHUNK, E5M2, "do%d" % c)
+            grouped = interleave(do_raw[c], do_plan[c][0:1], "do_bf%d" % c, do_plan[c][1])
+            codes, scales = quantize(grouped[:], DO_CHUNK, E5M2, "do%d" % c)
+            for n in range(per_chunk):
+                do_mx[c * per_chunk + n] = codes[:, n * P : (n + 1) * P], scales[:, n * P : (n + 1) * P]
 
-        do_first = cast_do(0)
+        def quantize_do_tile(i, grouped):
+            codes, scales = quantize(grouped[:], P, E5M2, "do_tile%d" % i)
+            do_mx[i] = codes[:], scales[:]
+
+        do_first = interleave(do_raw[0][:, :, 0:P], ("vector",), "do_bf_first", "v_pool3")
         v_codes, v_scales = quantize(v_bf[:], N, E4M3, "v")
-        do_mx[0] = quantize(do_first[:], DO_CHUNK, E5M2, "do0")
+        quantize_do_tile(0, do_first)
+        quantize_do_tile(1, interleave(do_raw[0][:, :, P : 2 * P], ("vector",), "do_bf_second", "v_bf"))
 
-        dp, ds_t, ds_mx = {}, {}, {}
+        dp, ds_t = {}, {}
 
         def multiply_values(i):
-            codes, scales = do_mx[i // per_chunk]
-            cols_i = slice((i % per_chunk) * P, (i % per_chunk + 1) * P)
-            dp[i] = bank("C" if i % 3 == 2 else "A", "dp")
+            codes, scales = do_mx[i]
+            dp[i] = bank(i % 3, "dp")
             nc.tensor.matmul_mx(
                 out=dp[i][:],
-                lhsT=codes[:, cols_i].bitcast(E5M2),
-                lhsT_scale=scales[:, cols_i],
+                lhsT=codes.bitcast(E5M2),
+                lhsT_scale=scales,
                 rhs=v_codes[:].bitcast(E4M3),
                 rhs_scale=v_scales[:],
                 start=True,
@@ -219,9 +259,9 @@ def tile_attend_gat_lse_q_ts_kernel(tc, qT, kT, vT, doT, lse, delta, rw, ts, off
 
         def make_ds(i):
             ds = ring.tile([P, N], BF16, name="ds", align_bytes=64)
-            nc.vector.scalar_tensor_tensor(ds[:], dp[i][:], cols[:, 12 + i : 13 + i], weights[i][:], ALU.subtract, ALU.mult)
+            nc.vector.scalar_tensor_tensor(ds[:], dp[i][:], cols[:, 4 + i : 5 + i], weights[i][:], ALU.subtract, ALU.mult)
             ds_words = ds[:].bitcast(F32)
-            ds_turned = bank("B", "ds_turned")
+            ds_turned = bank(3 + i % 2, "ds_turned")
             for u in range(2):
                 nc.tensor.transpose(ds_turned[:, u * P : (u + 1) * P], ds_words[:, u * P : (u + 1) * P], ident[:])
             ds_t[i] = ring.tile([P, N], BF16, name="ds_t", align_bytes=64)
@@ -232,7 +272,7 @@ def tile_attend_gat_lse_q_ts_kernel(tc, qT, kT, vT, doT, lse, delta, rw, ts, off
 
         def finish(i):
             codes, scales = quantize(ds_t[i][:], P, E5M2, "ds%d" % i, pool=ring, tag="dsq")
-            grad = bank("C", "grad")
+            grad = bank(5 + i % 3, "grad")
             nc.tensor.matmul_mx(
                 out=grad[:],
                 lhsT=codes[:].bitcast(E5M2),
@@ -243,19 +283,20 @@ def tile_attend_gat_lse_q_ts_kernel(tc, qT, kT, vT, doT, lse, delta, rw, ts, off
                 stop=True,
             )
             result = ring.tile([P, D], F32, name="result")
-            nc.scalar.activation(result[:], grad[:], ACT.Copy, scale=sign[:, 4 + i : 5 + i])
+            if i == TILES - 2:
+                nc.vector.tensor_scalar(result[:], grad[:], rw_sign[:, i : i + 1], None, ALU.mult)
+            else:
+                nc.scalar.activation(result[:], grad[:], ACT.Copy, scale=rw_sign[:, i : i + 1])
             nc.sync.dma_start(out=out[0, i * P : (i + 1) * P, :], in_=result[:])
 
         multiply_values(0)
         multiply_values(1)
-        prepare_do(1)
-        multiply_values(2)
         for i in range(TILES):
             make_ds(i)
-            if i in (0, 2):
-                prepare_do(i // per_chunk + 2)
-            if i + 3 < TILES:
-                multiply_values(i + 3)
+            if i % per_chunk == 0 and i // per_chunk + 1 < R // DO_CHUNK:
+                prepare_do(i // per_chunk + 1)
+            if i + 2 < TILES:
+                multiply_values(i + 2)
             if i >= 1:
                 finish(i - 1)
         finish(TILES - 1)

@@ -78,7 +78,9 @@ def tile_attend_gat_lse_q_ts_kernel(tc, qT, kT, vT, doT, lse, delta, rw, ts, off
             nc.sync.dma_start(out=rows[TILES * n : TILES * (n + 1), :], in_=vec[0].rearrange("(i m) o -> i (m o)", m=P))
         nc.sync.dma_start(out=ts_pool[0:1, :], in_=ts[0:1, :])
         k_pool.extend(load(k_view[:, j, :], "k_pool%d" % j) for j in range(1, PACK))
-        q_raw = [load(q_view[:, :, c * Q_CHUNK : (c + 1) * Q_CHUNK], "q_raw%d" % c) for c in range(R // Q_CHUNK)]
+        quarter = Q_CHUNK // 2
+        q_early = [load(q_view[:, :, n * quarter : (n + 1) * quarter], "q_early%d" % n) for n in range(2)]
+        q_late = load(q_view[:, :, Q_CHUNK:R], "q_late")
         v_pool = [load(v_view[:, j, :], "v_pool%d" % j) for j in range(PACK)]
         do_raw = [load(do_view[:, :, c * DO_CHUNK : (c + 1) * DO_CHUNK], "do_raw%d" % c) for c in range(R // DO_CHUNK)]
 
@@ -153,6 +155,7 @@ def tile_attend_gat_lse_q_ts_kernel(tc, qT, kT, vT, doT, lse, delta, rw, ts, off
         shift = keep.tile([P, 12], F32, name="shift", tag="k_pool3", align_bytes=64)
         nc.vector.tensor_reduce(shift[:], terms[:].rearrange("p g c -> p c g"), mybir.AxisListType.X, ALU.add)
         interleave_keys(1)
+        k_turned = turn_keys(1, 7)
         k_codes, k_scales = quantize(k_bf[:], N, E4M3, "k")
 
         per_half = Q_CHUNK // P
@@ -161,7 +164,7 @@ def tile_attend_gat_lse_q_ts_kernel(tc, qT, kT, vT, doT, lse, delta, rw, ts, off
         def score(half, q_mx):
             q_codes, q_scales = q_mx
             for j in range(PACK):
-                scores = bank((j + half) % PACK, "scores")
+                scores = bank(j, "scores")
                 nc.tensor.matmul_mx(
                     out=scores[:],
                     lhsT=k_codes[:, j * P : (j + 1) * P].bitcast(E4M3),
@@ -194,23 +197,22 @@ def tile_attend_gat_lse_q_ts_kernel(tc, qT, kT, vT, doT, lse, delta, rw, ts, off
                 )
                 weights.append(weight)
 
-        quarter = Q_CHUNK // 2
         q_first = (
             keep.tile([P, Q_CHUNK], U32, name="q0_codes", align_bytes=64),
-            keep.tile([P, Q_CHUNK], U8, name="q0_scales", align_bytes=64),
+            keep.tile([P, Q_CHUNK], U8, name="q0_scales", tag="k_bf", align_bytes=64),
         )
-        for n, (engine, tag) in enumerate((("vector", "stage"), ("scalar", "terms"))):
+        for n, tag in enumerate(("terms", "stage")):
             part = slice(n * quarter, (n + 1) * quarter)
-            grouped = interleave(q_raw[0][:, :, part], (engine,), "q_bf0_%d" % n, tag)
+            grouped = interleave(q_early[n], ("scalar",), "q_bf0_%d" % n, tag)
             nc.vector.quantize_mx(out=q_first[0][:, part].bitcast(E4M3), scales=q_first[1][:, part], in_=grouped[:])
+        sign_keys(1, k_turned)
+        ks_codes, ks_scales = quantize(ks_bf[:], D, E4M3, "ks")
         score(0, q_first)
-        q_second = quantize(interleave(q_raw[1], ("vector",), "q_bf1", "stage")[:], Q_CHUNK, E4M3, "q1")
-        sign_keys(1, turn_keys(1, 0))
+        q_second = quantize(interleave(q_late, ("vector",), "q_bf1", "stage")[:], Q_CHUNK, E4M3, "q1")
         turned_first = turn_logits(0)
         score(1, q_second)
         weigh(0, turned_first)
         weigh(1, turn_logits(1))
-        ks_codes, ks_scales = quantize(ks_bf[:], D, E4M3, "ks")
 
         v_picked = keep.tile([P, last * N], BF16, name="v_picked", tag="stage", align_bytes=64)
         for j in range(last):
@@ -225,7 +227,7 @@ def tile_attend_gat_lse_q_ts_kernel(tc, qT, kT, vT, doT, lse, delta, rw, ts, off
 
         do_mx = {}
         per_chunk = DO_CHUNK // P
-        do_plan = (None, ("scalar", "k_pool3"), ("scalar", "do_raw1"), ("vector", "do_raw2"))
+        do_plan = (None, ("scalar", "do_raw0"), ("vector", "do_raw1"), ("scalar", "do_raw2"))
 
         def prepare_do(c):
             grouped = interleave(do_raw[c], do_plan[c][0:1], "do_bf%d" % c, do_plan[c][1])
@@ -240,7 +242,7 @@ def tile_attend_gat_lse_q_ts_kernel(tc, qT, kT, vT, doT, lse, delta, rw, ts, off
         do_first = interleave(do_raw[0][:, :, 0:P], ("vector",), "do_bf_first", "v_pool3")
         v_codes, v_scales = quantize(v_bf[:], N, E4M3, "v")
         quantize_do_tile(0, do_first)
-        quantize_do_tile(1, interleave(do_raw[0][:, :, P : 2 * P], ("vector",), "do_bf_second", "v_bf"))
+        quantize_do_tile(1, interleave(do_raw[0][:, :, P : 2 * P], ("scalar",), "do_bf_second", "k_pool3"))
 
         dp, ds_t = {}, {}
 
@@ -282,7 +284,7 @@ def tile_attend_gat_lse_q_ts_kernel(tc, qT, kT, vT, doT, lse, delta, rw, ts, off
                 start=True,
                 stop=True,
             )
-            result = ring.tile([P, D], F32, name="result")
+            result = keep.tile([P, D], F32, name="result%d" % i)
             if i == TILES - 2:
                 nc.vector.tensor_scalar(result[:], grad[:], rw_sign[:, i : i + 1], None, ALU.mult)
             else:

@@ -39,10 +39,11 @@ def tile_attend_gat_lse_q_ts_kernel(tc, qT, kT, vT, doT, lse, delta, rw, ts, off
             nc.vector.quantize_mx(out=codes[:].bitcast(fmt), scales=scales[:], in_=src)
             return codes, scales
 
-        def interleave(raw, engines, name, tag):
+        def interleave(raw, engines, name, tag, grouped=None):
             width = raw.shape[2]
             share = width // len(engines)
-            grouped = keep.tile([P, width * PACK], BF16, name=name, tag=tag, align_bytes=64)
+            if grouped is None:
+                grouped = keep.tile([P, width * PACK], BF16, name=name, tag=tag, align_bytes=64)
             for n, engine in enumerate(engines):
                 dst = grouped[:, n * share * PACK : (n + 1) * share * PACK].rearrange("p (c i j) -> p c j i", i=4, j=PACK)
                 src = raw[:, :, n * share : (n + 1) * share].rearrange("p j (c i) -> p c j i", i=4)
@@ -66,7 +67,8 @@ def tile_attend_gat_lse_q_ts_kernel(tc, qT, kT, vT, doT, lse, delta, rw, ts, off
         rows = keep.tile([P, P], F32, name="rows")
         nc.vector.memset(rows[:], 0.0)
         ts_pool = keep.tile([P, T], F32, name="ts_pool")
-        nc.vector.memset(ts_pool[:], 0.0)
+        nc.vector.memset(ts_pool[:, 0 : T // 2], 0.0)
+        nc.gpsimd.memset(ts_pool[:, T // 2 : T], 0.0)
         ident = keep.tile([P, P], F32, name="ident")
         make_identity(nc, ident[:])
         warm_ln = keep.tile([P, 1], F32, name="warm_ln")
@@ -117,6 +119,12 @@ def tile_attend_gat_lse_q_ts_kernel(tc, qT, kT, vT, doT, lse, delta, rw, ts, off
         nc.gpsimd.tensor_scalar(parts[:, 2, :], absolute[:], 2.0**-63, 2.0**-126, ALU.min, ALU.max)
         nc.scalar.activation(terms[:, 0:2, :], parts[:, 0:2, :], ACT.Ln)
         nc.scalar.activation(terms[:, 2, :], parts[:, 2, :], ACT.Ln, scale=2.0**63)
+        sums = keep.tile([P, 2, 12], F32, name="sums")
+        nc.gpsimd.tensor_tensor(sums[:], terms[:, 0:2, :], terms[:, 2:4, :], ALU.add)
+        shift = keep.tile([P, 12], F32, name="shift", tag="shift", align_bytes=64)
+        nc.gpsimd.tensor_tensor(shift[:], sums[:, 0, :], sums[:, 1, :], ALU.add)
+        shift_late = keep.tile([P, 1], F32, name="shift_late", tag="shift_late", align_bytes=64)
+        nc.gpsimd.tensor_tensor(shift_late[:], sums[:, 0, 4:5], sums[:, 1, 4:5], ALU.add)
         warm = keep.tile([P, 1], F32, name="warm")
         nc.scalar.activation(warm[:], terms[:, 2, 0:1], ACT.Exp)
 
@@ -128,13 +136,21 @@ def tile_attend_gat_lse_q_ts_kernel(tc, qT, kT, vT, doT, lse, delta, rw, ts, off
                 nc.tensor.transpose(turned[:, w * P : (w + 1) * P], words[:, first + w % 2 : first + 2 * P : 2], ident[:])
             return turned
 
-        def sign_keys(a, turned):
+        ks_codes = keep.tile([P, D], U32, name="ks_codes", align_bytes=64)
+        ks_scales = keep.tile([P, D], U8, name="ks_scales", align_bytes=64)
+
+        def sign_keys(turned, signed):
             nc.vector.tensor_tensor(
-                ks_bf[:].rearrange("s (p a w e) -> s a p w e", a=2, w=4, e=2)[:, a],
+                signed[:].rearrange("s (p w e) -> s p w e", w=4, e=2),
                 turned[:].bitcast(BF16).rearrange("s (w p e) -> s p w e", w=4, e=2),
                 ts_sign[:].rearrange("s j (u e) -> s (j u) e", e=2).unsqueeze(1).to_broadcast([P, P, 4, 2]),
                 ALU.mult,
             )
+            return signed
+
+        def quantize_signed(a, signed):
+            part = slice(a * D // 2, (a + 1) * D // 2)
+            nc.vector.quantize_mx(out=ks_codes[:, part].bitcast(E4M3), scales=ks_scales[:, part], in_=signed[:])
 
         k_bf = keep.tile([P, N * PACK], BF16, name="k_bf", tag="k_bf", align_bytes=64)
 
@@ -149,14 +165,25 @@ def tile_attend_gat_lse_q_ts_kernel(tc, qT, kT, vT, doT, lse, delta, rw, ts, off
         k_turned = turn_keys(0, 6)
         interleave_keys(0)
         gather_keys(2)
-        ks_bf = keep.tile([P, D * PACK], BF16, name="ks_bf", tag="k_pool2", align_bytes=64)
-        sign_keys(0, k_turned)
+        signed_first = sign_keys(k_turned, keep.tile([P, 2 * N], BF16, name="signed0", tag="k_pool2", align_bytes=64))
         gather_keys(3)
-        shift = keep.tile([P, 12], F32, name="shift", tag="k_pool3", align_bytes=64)
-        nc.vector.tensor_reduce(shift[:], terms[:].rearrange("p g c -> p c g"), mybir.AxisListType.X, ALU.add)
         interleave_keys(1)
         k_turned = turn_keys(1, 7)
         k_codes, k_scales = quantize(k_bf[:], N, E4M3, "k")
+
+        def warm_up(number):
+            nc.tensor.matmul_mx(
+                out=bank(number, "unread")[:],
+                lhsT=k_codes[:, 0:P].bitcast(E4M3),
+                lhsT_scale=k_scales[:, 0:P],
+                rhs=k_codes[:].bitcast(E4M3),
+                rhs_scale=k_scales[:],
+                start=True,
+                stop=True,
+            )
+
+        warm_up(4)
+        warm_up(5)
 
         per_half = Q_CHUNK // P
         logits, weights = {}, []
@@ -185,36 +212,57 @@ def tile_attend_gat_lse_q_ts_kernel(tc, qT, kT, vT, doT, lse, delta, rw, ts, off
                     nc.tensor.transpose(turned[m][:, j * P : (j + 1) * P], logits[half, j][:, m * P : (m + 1) * P], ident[:])
             return turned
 
+        do_mx, do_bf = {}, {}
+        per_chunk = DO_CHUNK // P
+
+        def cast_do(first, count, engine, tag):
+            c, n = divmod(first, per_chunk)
+            do_bf[first] = interleave(do_raw[c][:, :, n * P : (n + count) * P], (engine,), "do_bf%d" % first, tag)
+
+        def quantize_do(first, count, tag):
+            codes = keep.tile([P, count * P], U32, name="do%d_codes" % first, tag=tag, align_bytes=64)
+            scales = keep.tile([P, count * P], U8, name="do%d_scales" % first, align_bytes=64)
+            nc.vector.quantize_mx(out=codes[:].bitcast(E5M2), scales=scales[:], in_=do_bf[first][:])
+            for n in range(count):
+                do_mx[first + n] = codes[:, n * P : (n + 1) * P], scales[:, n * P : (n + 1) * P]
+
         def weigh(half, turned):
             for m in range(per_half):
                 i = half * per_half + m
-                weight = keep.tile([P, N], F32, name="weight%d" % i, align_bytes=64)
+                weight = keep.tile([P, N], F32, name="weight%d" % i, tag="weight%d" % i, align_bytes=64)
                 nc.scalar.activation(
                     weight[:].rearrange("p (u s e) -> p u s e", u=2, e=2),
                     turned[m][:].rearrange("p (u e s) -> p u s e", u=2, e=2),
                     ACT.Exp,
-                    bias=shift[:, i : i + 1],
+                    bias=shift_late[:] if i == per_half else shift[:, i : i + 1],
                 )
                 weights.append(weight)
+                if i == per_half:
+                    cast_do(0, 1, "scalar", "shift_late")
 
         q_first = (
             keep.tile([P, Q_CHUNK], U32, name="q0_codes", align_bytes=64),
             keep.tile([P, Q_CHUNK], U8, name="q0_scales", tag="k_bf", align_bytes=64),
         )
-        for n, tag in enumerate(("terms", "stage")):
+        stage = keep.tile([P, 6 * N], BF16, name="stage", align_bytes=64)
+        for n, place in enumerate((None, stage[:, 3 * N : 5 * N])):
             part = slice(n * quarter, (n + 1) * quarter)
-            grouped = interleave(q_early[n], ("scalar",), "q_bf0_%d" % n, tag)
+            grouped = interleave(q_early[n], ("scalar",), "q_bf0_%d" % n, "terms", place)
             nc.vector.quantize_mx(out=q_first[0][:, part].bitcast(E4M3), scales=q_first[1][:, part], in_=grouped[:])
-        sign_keys(1, k_turned)
-        ks_codes, ks_scales = quantize(ks_bf[:], D, E4M3, "ks")
         score(0, q_first)
-        q_second = quantize(interleave(q_late, ("vector",), "q_bf1", "stage")[:], Q_CHUNK, E4M3, "q1")
+        q_bf1 = interleave(q_late, ("vector",), "q_bf1", None, stage[:, 0 : 4 * N])
+        signed_second = sign_keys(k_turned, stage[:, 4 * N : 6 * N])
+        q_second = quantize(q_bf1[:], Q_CHUNK, E4M3, "q1")
+        quantize_signed(0, signed_first)
+        quantize_signed(1, signed_second)
         turned_first = turn_logits(0)
         score(1, q_second)
         weigh(0, turned_first)
         weigh(1, turn_logits(1))
+        for number in (4, 4):
+            warm_up(number)
 
-        v_picked = keep.tile([P, last * N], BF16, name="v_picked", tag="stage", align_bytes=64)
+        v_picked = stage[:, N : 4 * N]
         for j in range(last):
             nc.vector.tensor_copy(out=v_picked[:, j * N : (j + 1) * N], in_=v_pool[j][:].indirect(offsets[:]))
         v_bf = keep.tile([P, N * PACK], BF16, name="v_bf", tag="v_bf", align_bytes=64)
@@ -225,30 +273,18 @@ def tile_attend_gat_lse_q_ts_kernel(tc, qT, kT, vT, doT, lse, delta, rw, ts, off
         )
         nc.vector.tensor_copy(out=v_places[:, :, last], in_=v_pool[last][:].indirect(offsets[:]))
 
-        do_mx = {}
-        per_chunk = DO_CHUNK // P
-        do_plan = (None, ("scalar", "do_raw0"), ("vector", "do_raw1"), ("scalar", "do_raw2"))
-
-        def prepare_do(c):
-            grouped = interleave(do_raw[c], do_plan[c][0:1], "do_bf%d" % c, do_plan[c][1])
-            codes, scales = quantize(grouped[:], DO_CHUNK, E5M2, "do%d" % c)
-            for n in range(per_chunk):
-                do_mx[c * per_chunk + n] = codes[:, n * P : (n + 1) * P], scales[:, n * P : (n + 1) * P]
-
-        def quantize_do_tile(i, grouped):
-            codes, scales = quantize(grouped[:], P, E5M2, "do_tile%d" % i)
-            do_mx[i] = codes[:], scales[:]
-
-        do_first = interleave(do_raw[0][:, :, 0:P], ("vector",), "do_bf_first", "v_pool3")
+        quantize_do(0, 1, "v_pool3")
         v_codes, v_scales = quantize(v_bf[:], N, E4M3, "v")
-        quantize_do_tile(0, do_first)
-        quantize_do_tile(1, interleave(do_raw[0][:, :, P : 2 * P], ("scalar",), "do_bf_second", "k_pool3"))
+        cast_do(1, 1, "vector", "v_bf")
+        quantize_do(1, 1, "do1_codes")
+        cast_do(2, 2, "scalar", "shift")
+        cast_do(4, 2, "scalar", "do_raw1")
 
         dp, ds_t = {}, {}
 
         def multiply_values(i):
             codes, scales = do_mx[i]
-            dp[i] = bank(i % 3, "dp")
+            dp[i] = bank((0, 1, 2, 7)[i % 4], "dp")
             nc.tensor.matmul_mx(
                 out=dp[i][:],
                 lhsT=codes.bitcast(E5M2),
@@ -260,13 +296,13 @@ def tile_attend_gat_lse_q_ts_kernel(tc, qT, kT, vT, doT, lse, delta, rw, ts, off
             )
 
         def make_ds(i):
-            ds = ring.tile([P, N], BF16, name="ds", align_bytes=64)
+            ds = keep.tile([P, N], BF16, name="ds%d" % i, tag="ds%d" % i, align_bytes=64)
             nc.vector.scalar_tensor_tensor(ds[:], dp[i][:], cols[:, 4 + i : 5 + i], weights[i][:], ALU.subtract, ALU.mult)
             ds_words = ds[:].bitcast(F32)
             ds_turned = bank(3 + i % 2, "ds_turned")
             for u in range(2):
                 nc.tensor.transpose(ds_turned[:, u * P : (u + 1) * P], ds_words[:, u * P : (u + 1) * P], ident[:])
-            ds_t[i] = ring.tile([P, N], BF16, name="ds_t", align_bytes=64)
+            ds_t[i] = keep.tile([P, N], BF16, name="ds_t%d" % i, tag="ds_t%d" % i, align_bytes=64)
             nc.scalar.copy(
                 out=ds_t[i][:].bitcast(F32).rearrange("s (r u) -> s r u", u=2),
                 in_=ds_turned[:, 0 : 2 * P].rearrange("s (u r) -> s r u", u=2),
@@ -274,7 +310,7 @@ def tile_attend_gat_lse_q_ts_kernel(tc, qT, kT, vT, doT, lse, delta, rw, ts, off
 
         def finish(i):
             codes, scales = quantize(ds_t[i][:], P, E5M2, "ds%d" % i, pool=ring, tag="dsq")
-            grad = bank(5 + i % 3, "grad")
+            grad = bank(5 + i % 2, "grad")
             nc.tensor.matmul_mx(
                 out=grad[:],
                 lhsT=codes[:].bitcast(E5M2),
@@ -285,20 +321,30 @@ def tile_attend_gat_lse_q_ts_kernel(tc, qT, kT, vT, doT, lse, delta, rw, ts, off
                 stop=True,
             )
             result = keep.tile([P, D], F32, name="result%d" % i)
+            ordered = result[:].rearrange("r (p a j) -> r p a j", a=2, j=2)
+            halves = grad[:].rearrange("r (a p j) -> r p a j", a=2, j=2)
             if i == TILES - 2:
-                nc.vector.tensor_scalar(result[:], grad[:], rw_sign[:, i : i + 1], None, ALU.mult)
+                nc.vector.tensor_scalar(ordered, halves, rw_sign[:, i : i + 1], None, ALU.mult)
             else:
-                nc.scalar.activation(result[:], grad[:], ACT.Copy, scale=rw_sign[:, i : i + 1])
+                nc.scalar.activation(ordered, halves, ACT.Copy, scale=rw_sign[:, i : i + 1])
             nc.sync.dma_start(out=out[0, i * P : (i + 1) * P, :], in_=result[:])
 
-        multiply_values(0)
-        multiply_values(1)
+        for i in range(2):
+            multiply_values(i)
         for i in range(TILES):
             make_ds(i)
-            if i % per_chunk == 0 and i // per_chunk + 1 < R // DO_CHUNK:
-                prepare_do(i // per_chunk + 1)
-            if i + 2 < TILES:
-                multiply_values(i + 2)
-            if i >= 1:
-                finish(i - 1)
+            if i == 0:
+                quantize_do(2, 2, "do2_codes")
+                multiply_values(2)
+            if i == 1:
+                quantize_do(4, 2, "weight0")
+            if i in (3, 4):
+                quantize_do(i + 3, 1, "weight%d" % (i - 1))
+            if i + 3 < TILES:
+                multiply_values(i + 3)
+            if i >= 2:
+                finish(i - 2)
+            if i in (0, 1):
+                cast_do(i + 6, 1, "scalar", "ds%d" % i)
+        finish(TILES - 2)
         finish(TILES - 1)

@@ -308,11 +308,13 @@ def tile_attend_gat_lse_q_ts_kernel(tc, qT, kT, vT, doT, lse, delta, rw, ts, off
                 in_=ds_turned[:, 0 : 2 * P].rearrange("s (u r) -> s r u", u=2),
             )
 
-        def finish(i):
+        grad = {}
+
+        def multiply_keys(i):
             codes, scales = quantize(ds_t[i][:], P, E5M2, "ds%d" % i, pool=ring, tag="dsq")
-            grad = bank(5 + i % 2, "grad")
+            grad[i] = bank(5 + i % 2 if i < TILES - 2 else i % 2, "grad")
             nc.tensor.matmul_mx(
-                out=grad[:],
+                out=grad[i][:],
                 lhsT=codes[:].bitcast(E5M2),
                 lhsT_scale=scales[:],
                 rhs=ks_codes[:].bitcast(E4M3),
@@ -320,14 +322,18 @@ def tile_attend_gat_lse_q_ts_kernel(tc, qT, kT, vT, doT, lse, delta, rw, ts, off
                 start=True,
                 stop=True,
             )
-            result = keep.tile([P, D], F32, name="result%d" % i)
-            ordered = result[:].rearrange("r (p a j) -> r p a j", a=2, j=2)
-            halves = grad[:].rearrange("r (a p j) -> r p a j", a=2, j=2)
-            if i == TILES - 2:
-                nc.vector.tensor_scalar(ordered, halves, rw_sign[:, i : i + 1], None, ALU.mult)
-            else:
-                nc.scalar.activation(ordered, halves, ACT.Copy, scale=rw_sign[:, i : i + 1])
-            nc.sync.dma_start(out=out[0, i * P : (i + 1) * P, :], in_=result[:])
+
+        def store(i, engine, parts=1):
+            width = D // parts
+            for n in range(parts):
+                result = keep.tile([P, width], F32, name="result%d_%d" % (i, n))
+                ordered = result[:].rearrange("r (p a j) -> r p a j", a=2, j=2)
+                halves = grad[i][:].rearrange("r (a p j) -> r p a j", a=2, j=2)[:, n * width // PACK : (n + 1) * width // PACK]
+                if engine == "vector":
+                    nc.vector.tensor_scalar(ordered, halves, rw_sign[:, i : i + 1], None, ALU.mult)
+                else:
+                    nc.scalar.activation(ordered, halves, ACT.Copy, scale=rw_sign[:, i : i + 1])
+                nc.sync.dma_start(out=out[0, i * P : (i + 1) * P, n * width : (n + 1) * width], in_=result[:])
 
         for i in range(2):
             multiply_values(i)
@@ -343,8 +349,14 @@ def tile_attend_gat_lse_q_ts_kernel(tc, qT, kT, vT, doT, lse, delta, rw, ts, off
             if i + 3 < TILES:
                 multiply_values(i + 3)
             if i >= 2:
-                finish(i - 2)
+                multiply_keys(i - 2)
+            if 2 <= i < TILES - 2:
+                store(i - 2, "scalar")
             if i in (0, 1):
                 cast_do(i + 6, 1, "scalar", "ds%d" % i)
-        finish(TILES - 2)
-        finish(TILES - 1)
+        multiply_keys(6)
+        store(4, "vector")
+        multiply_keys(7)
+        store(5, "scalar")
+        store(6, "vector")
+        store(7, "scalar", parts=2)

@@ -262,20 +262,14 @@ def tile_attend_gat_lse_q_ts_kernel(tc, qT, kT, vT, doT, lse, delta, rw, ts, off
         for number in (4, 4):
             warm_up(number)
 
-        v_picked = stage[:, N : 4 * N]
-        for j in range(last):
-            nc.vector.tensor_copy(out=v_picked[:, j * N : (j + 1) * N], in_=v_pool[j][:].indirect(offsets[:]))
-        v_bf = keep.tile([P, N * PACK], BF16, name="v_bf", tag="v_bf", align_bytes=64)
-        v_places = v_bf[:].rearrange("p (u s e j) -> p s j u e", u=2, e=2, j=PACK)
-        nc.vector.tensor_copy(
-            out=v_places[:, :, 0:last],
-            in_=v_picked[:].rearrange("p (j s u e) -> p s j u e", j=last, u=2, e=2),
-        )
-        nc.vector.tensor_copy(out=v_places[:, :, last], in_=v_pool[last][:].indirect(offsets[:]))
+        v_bf = keep.tile([P, PACK * N], BF16, name="v_bf", tag="q_late", align_bytes=64)[:]
+        v_places = v_bf.rearrange("p (u s e j) -> p s j u e", u=2, e=2, j=PACK)
+        for j in range(PACK):
+            nc.vector.tensor_copy(out=v_places[:, :, j], in_=v_pool[j][:].indirect(offsets[:]))
 
-        quantize_do(0, 1, "v_pool3")
-        v_codes, v_scales = quantize(v_bf[:], N, E4M3, "v")
-        cast_do(1, 1, "vector", "v_bf")
+        v_codes, v_scales = quantize(v_bf, N, E4M3, "v")
+        quantize_do(0, 1, "q_late")
+        cast_do(1, 1, "vector", "shift_late")
         quantize_do(1, 1, "do1_codes")
         cast_do(2, 2, "scalar", "shift")
         cast_do(4, 2, "scalar", "do_raw1")

@@ -123,8 +123,6 @@ def tile_attend_gat_lse_q_ts_kernel(tc, qT, kT, vT, doT, lse, delta, rw, ts, off
         nc.gpsimd.tensor_tensor(sums[:], terms[:, 0:2, :], terms[:, 2:4, :], ALU.add)
         shift = keep.tile([P, 12], F32, name="shift", tag="shift", align_bytes=64)
         nc.gpsimd.tensor_tensor(shift[:], sums[:, 0, :], sums[:, 1, :], ALU.add)
-        shift_late = keep.tile([P, 1], F32, name="shift_late", tag="shift_late", align_bytes=64)
-        nc.gpsimd.tensor_tensor(shift_late[:], sums[:, 0, 4:5], sums[:, 1, 4:5], ALU.add)
         warm = keep.tile([P, 1], F32, name="warm")
         nc.scalar.activation(warm[:], terms[:, 2, 0:1], ACT.Exp)
 
@@ -234,11 +232,9 @@ def tile_attend_gat_lse_q_ts_kernel(tc, qT, kT, vT, doT, lse, delta, rw, ts, off
                     weight[:].rearrange("p (u s e) -> p u s e", u=2, e=2),
                     turned[m][:].rearrange("p (u e s) -> p u s e", u=2, e=2),
                     ACT.Exp,
-                    bias=shift_late[:] if i == per_half else shift[:, i : i + 1],
+                    bias=shift[:, i : i + 1],
                 )
                 weights.append(weight)
-                if i == per_half:
-                    cast_do(0, 1, "scalar", "shift_late")
 
         q_first = (
             keep.tile([P, Q_CHUNK], U32, name="q0_codes", align_bytes=64),
@@ -267,9 +263,10 @@ def tile_attend_gat_lse_q_ts_kernel(tc, qT, kT, vT, doT, lse, delta, rw, ts, off
         for j in range(PACK):
             nc.vector.tensor_copy(out=v_places[:, :, j], in_=v_pool[j][:].indirect(offsets[:]))
 
+        cast_do(0, 1, "vector", "v_pool3")
         v_codes, v_scales = quantize(v_bf, N, E4M3, "v")
-        quantize_do(0, 1, "q_late")
-        cast_do(1, 1, "vector", "shift_late")
+        quantize_do(0, 1, "do0_codes")
+        cast_do(1, 1, "vector", "q_late")
         quantize_do(1, 1, "do1_codes")
         cast_do(2, 2, "scalar", "shift")
         cast_do(4, 2, "scalar", "do_raw1")

@@ -20,7 +20,7 @@ P = 128
 PACK = 4
 TILES = R // P
 Q_CHUNK = 512
-DO_CHUNK = 256
+DO_LOADS = ((1, 2), (3, 2), (5, 2), (7, 1))
 
 
 def tile_attend_gat_lse_q_ts_kernel(tc, qT, kT, vT, doT, lse, delta, rw, ts, offs, out):
@@ -28,6 +28,7 @@ def tile_attend_gat_lse_q_ts_kernel(tc, qT, kT, vT, doT, lse, delta, rw, ts, off
     with ExitStack() as ctx:
         keep = ctx.enter_context(tc.tile_pool(name="keep", bufs=1))
         ring = ctx.enter_context(tc.tile_pool(name="ring", bufs=4))
+        reuse = ctx.enter_context(tc.tile_pool(name="reuse", bufs=1))
         psum = ctx.enter_context(tc.psum_pool(name="psum", bufs=1))
 
         def bank(number, name):
@@ -80,11 +81,16 @@ def tile_attend_gat_lse_q_ts_kernel(tc, qT, kT, vT, doT, lse, delta, rw, ts, off
             nc.sync.dma_start(out=rows[TILES * n : TILES * (n + 1), :], in_=vec[0].rearrange("(i m) o -> i (m o)", m=P))
         nc.sync.dma_start(out=ts_pool[0:1, :], in_=ts[0:1, :])
         k_pool.extend(load(k_view[:, j, :], "k_pool%d" % j) for j in range(1, PACK))
-        quarter = Q_CHUNK // 2
-        q_early = [load(q_view[:, :, n * quarter : (n + 1) * quarter], "q_early%d" % n) for n in range(2)]
+        q_early = load(q_view[:, :, 0:Q_CHUNK], "q_early")
         q_late = load(q_view[:, :, Q_CHUNK:R], "q_late")
         v_pool = [load(v_view[:, j, :], "v_pool%d" % j) for j in range(PACK)]
-        do_raw = [load(do_view[:, :, c * DO_CHUNK : (c + 1) * DO_CHUNK], "do_raw%d" % c) for c in range(R // DO_CHUNK)]
+        do_first = reuse.tile([P, PACK, P], F32, name="do_first", align_bytes=64, offset=0)
+        nc.sync.dma_start(out=do_first[:], in_=do_view[:, :, 0:P])
+        do_raw = {0: do_first}
+        for first, count in DO_LOADS:
+            raw = load(do_view[:, :, first * P : (first + count) * P], "do_raw%d" % first)
+            for n in range(count):
+                do_raw[first + n] = raw[:, :, n * P : (n + 1) * P]
 
         k_pairs = [keep.tile([P, 2 * N], BF16, name="k_pair%d" % a, align_bytes=64) for a in range(2)]
 
@@ -134,7 +140,7 @@ def tile_attend_gat_lse_q_ts_kernel(tc, qT, kT, vT, doT, lse, delta, rw, ts, off
                 nc.tensor.transpose(turned[:, w * P : (w + 1) * P], words[:, first + w % 2 : first + 2 * P : 2], ident[:])
             return turned
 
-        ks_codes = keep.tile([P, D], U32, name="ks_codes", align_bytes=64)
+        ks_codes = keep.tile([P, D], U32, name="ks_codes", tag="k_pool3", align_bytes=64)
         ks_scales = keep.tile([P, D], U8, name="ks_scales", align_bytes=64)
 
         def sign_keys(turned, signed):
@@ -168,108 +174,110 @@ def tile_attend_gat_lse_q_ts_kernel(tc, qT, kT, vT, doT, lse, delta, rw, ts, off
         interleave_keys(1)
         k_turned = turn_keys(1, 7)
         k_codes, k_scales = quantize(k_bf[:], N, E4M3, "k")
+        quantize_signed(0, signed_first)
 
-        def warm_up(number):
+        def warm_up(target, codes, scales):
             nc.tensor.matmul_mx(
-                out=bank(number, "unread")[:],
-                lhsT=k_codes[:, 0:P].bitcast(E4M3),
-                lhsT_scale=k_scales[:, 0:P],
-                rhs=k_codes[:].bitcast(E4M3),
-                rhs_scale=k_scales[:],
+                out=target,
+                lhsT=codes[:, 0:P].bitcast(E4M3),
+                lhsT_scale=scales[:, 0:P],
+                rhs=codes.bitcast(E4M3),
+                rhs_scale=scales,
                 start=True,
                 stop=True,
             )
 
-        warm_up(4)
-        warm_up(5)
+        for number in (4, 5):
+            unread = bank(number, "unread")
+            for n in range(2):
+                warm_up(unread[:, n * D // 2 : (n + 1) * D // 2], ks_codes[:, 0 : D // 2], ks_scales[:, 0 : D // 2])
 
         per_half = Q_CHUNK // P
         logits, weights = {}, []
 
-        def score(half, q_mx):
+        def score(half, q_mx, rows_in=slice(0, Q_CHUNK)):
             q_codes, q_scales = q_mx
             for j in range(PACK):
                 scores = bank(j, "scores")
                 nc.tensor.matmul_mx(
-                    out=scores[:],
+                    out=scores[:, rows_in],
                     lhsT=k_codes[:, j * P : (j + 1) * P].bitcast(E4M3),
                     lhsT_scale=k_scales[:, j * P : (j + 1) * P],
-                    rhs=q_codes[:].bitcast(E4M3),
-                    rhs_scale=q_scales[:],
+                    rhs=q_codes[:, rows_in].bitcast(E4M3),
+                    rhs_scale=q_scales[:, rows_in],
                     start=True,
                     stop=True,
                 )
-                logit = keep.tile([P, Q_CHUNK], F32, name="logit%d_%d" % (half, j), align_bytes=64)
-                nc.scalar.activation(logit[:], scores[:], ACT.Identity, bias=shift[:, 8 + j : 9 + j], scale=cols[:, j : j + 1])
-                logits[half, j] = logit
-
-        def turn_logits(half):
-            turned = [bank(4 + m, "turned%d" % m) for m in range(per_half)]
-            for j in range(PACK):
-                for m in range(per_half):
-                    nc.tensor.transpose(turned[m][:, j * P : (j + 1) * P], logits[half, j][:, m * P : (m + 1) * P], ident[:])
-            return turned
+                if (half, j) not in logits:
+                    logits[half, j] = keep.tile([P, Q_CHUNK], F32, name="logit%d_%d" % (half, j), tag="logit%d_%d" % (half, j), align_bytes=64)
+                nc.scalar.activation(
+                    logits[half, j][:, rows_in], scores[:, rows_in], ACT.Identity, bias=shift[:, 8 + j : 9 + j], scale=cols[:, j : j + 1]
+                )
 
         do_mx, do_bf = {}, {}
-        per_chunk = DO_CHUNK // P
 
-        def cast_do(first, count, engine, tag):
-            c, n = divmod(first, per_chunk)
-            do_bf[first] = interleave(do_raw[c][:, :, n * P : (n + count) * P], (engine,), "do_bf%d" % first, tag)
+        def cast_do(i, engine, tag=None):
+            do_bf[i] = interleave(do_raw[i], (engine,), "do_bf%d" % i, tag or "do_bf%d" % i)
 
-        def quantize_do(first, count, tag):
-            codes = keep.tile([P, count * P], U32, name="do%d_codes" % first, tag=tag, align_bytes=64)
-            scales = keep.tile([P, count * P], U8, name="do%d_scales" % first, align_bytes=64)
-            nc.vector.quantize_mx(out=codes[:].bitcast(E5M2), scales=scales[:], in_=do_bf[first][:])
-            for n in range(count):
-                do_mx[first + n] = codes[:, n * P : (n + 1) * P], scales[:, n * P : (n + 1) * P]
+        def quantize_do(i):
+            do_mx[i] = quantize(do_bf[i][:], P, E5M2, "do%d" % i)
 
-        def weigh(half, turned):
-            for m in range(per_half):
+        def weigh(half, members, places=None):
+            for m in members:
                 i = half * per_half + m
-                weight = keep.tile([P, N], F32, name="weight%d" % i, tag="weight%d" % i, align_bytes=64)
+                turned = bank(4 + m, "turned")
+                for j in range(PACK):
+                    nc.tensor.transpose(turned[:, j * P : (j + 1) * P], logits[half, j][:, m * P : (m + 1) * P], ident[:])
+                if places is None:
+                    weight = keep.tile([P, N], F32, name="weight%d" % i, tag="weight%d" % i, align_bytes=64)
+                else:
+                    weight = places[:, m % 2 * N : (m % 2 + 1) * N]
                 nc.scalar.activation(
                     weight[:].rearrange("p (u s e) -> p u s e", u=2, e=2),
-                    turned[m][:].rearrange("p (u e s) -> p u s e", u=2, e=2),
+                    turned[:].rearrange("p (u e s) -> p u s e", u=2, e=2),
                     ACT.Exp,
                     bias=shift[:, i : i + 1],
                 )
                 weights.append(weight)
 
+        quarter = Q_CHUNK // 2
         q_first = (
-            keep.tile([P, Q_CHUNK], U32, name="q0_codes", align_bytes=64),
-            keep.tile([P, Q_CHUNK], U8, name="q0_scales", tag="k_bf", align_bytes=64),
+            keep.tile([P, Q_CHUNK], U32, name="q0_codes", tag="q_early", align_bytes=64),
+            keep.tile([P, Q_CHUNK], U8, name="q0_scales", align_bytes=64),
         )
-        stage = keep.tile([P, 6 * N], BF16, name="stage", align_bytes=64)
-        for n, place in enumerate((None, stage[:, 3 * N : 5 * N])):
-            part = slice(n * quarter, (n + 1) * quarter)
-            grouped = interleave(q_early[n], ("scalar",), "q_bf0_%d" % n, "terms", place)
+        parts_q = [slice(n * quarter, (n + 1) * quarter) for n in range(2)]
+        q_bf0 = [
+            interleave(q_early[:, :, part], (engine,), "q_bf0_%s" % engine, "q_bf0_%s" % engine)
+            for part, engine in zip(parts_q, ("scalar", "vector"))
+        ]
+        for part, grouped in zip(parts_q, q_bf0):
             nc.vector.quantize_mx(out=q_first[0][:, part].bitcast(E4M3), scales=q_first[1][:, part], in_=grouped[:])
-        score(0, q_first)
-        q_bf1 = interleave(q_late, ("vector",), "q_bf1", None, stage[:, 0 : 4 * N])
-        signed_second = sign_keys(k_turned, stage[:, 4 * N : 6 * N])
+        for part in parts_q:
+            score(0, q_first, part)
+        signed_second = sign_keys(k_turned, keep.tile([P, 2 * N], BF16, name="signed1", tag="q_bf0_scalar", align_bytes=64))
+        q_bf1 = interleave(q_late, ("vector",), "q_bf1", "q_bf1")
         q_second = quantize(q_bf1[:], Q_CHUNK, E4M3, "q1")
-        quantize_signed(0, signed_first)
         quantize_signed(1, signed_second)
-        turned_first = turn_logits(0)
+        weigh(0, (0, 1))
         score(1, q_second)
-        weigh(0, turned_first)
-        weigh(1, turn_logits(1))
-        for number in (4, 4):
-            warm_up(number)
+        weigh(0, (2, 3))
+        weigh(1, (0, 1))
+        cast_do(0, "scalar")
+        weigh(1, (2, 3), reuse.tile([P, 2 * N], F32, name="last_weights", align_bytes=64, offset=1024))
+        for number in (4, 5):
+            warm_up(bank(number, "unread")[:], k_codes[:], k_scales[:])
 
         v_bf = keep.tile([P, PACK * N], BF16, name="v_bf", tag="q_late", align_bytes=64)[:]
         v_places = v_bf.rearrange("p (u s e j) -> p s j u e", u=2, e=2, j=PACK)
         for j in range(PACK):
             nc.vector.tensor_copy(out=v_places[:, :, j], in_=v_pool[j][:].indirect(offsets[:]))
 
-        cast_do(0, 1, "vector", "v_pool3")
-        v_codes, v_scales = quantize(v_bf, N, E4M3, "v")
-        quantize_do(0, 1, "do0_codes")
-        cast_do(1, 1, "vector", "q_late")
-        quantize_do(1, 1, "do1_codes")
-        cast_do(2, 2, "scalar", "shift")
-        cast_do(4, 2, "scalar", "do_raw1")
+        quantize_do(0)
+        v_codes = keep.tile([P, N], U32, name="v_codes", align_bytes=64)
+        v_scales = reuse.tile([P, N], U8, name="v_scales", align_bytes=64, offset=0)
+        nc.vector.quantize_mx(out=v_codes[:].bitcast(E4M3), scales=v_scales[:], in_=v_bf)
+        cast_do(1, "vector")
+        quantize_do(1)
 
         dp, ds_t = {}, {}
 
@@ -278,32 +286,36 @@ def tile_attend_gat_lse_q_ts_kernel(tc, qT, kT, vT, doT, lse, delta, rw, ts, off
             dp[i] = bank((0, 1, 2, 7)[i % 4], "dp")
             nc.tensor.matmul_mx(
                 out=dp[i][:],
-                lhsT=codes.bitcast(E5M2),
-                lhsT_scale=scales,
+                lhsT=codes[:].bitcast(E5M2),
+                lhsT_scale=scales[:],
                 rhs=v_codes[:].bitcast(E4M3),
                 rhs_scale=v_scales[:],
                 start=True,
                 stop=True,
             )
 
+        ds_turned = {}
+
         def make_ds(i):
             ds = keep.tile([P, N], BF16, name="ds%d" % i, tag="ds%d" % i, align_bytes=64)
             nc.vector.scalar_tensor_tensor(ds[:], dp[i][:], cols[:, 4 + i : 5 + i], weights[i][:], ALU.subtract, ALU.mult)
             ds_words = ds[:].bitcast(F32)
-            ds_turned = bank(3 + i % 2, "ds_turned")
+            ds_turned[i] = bank(3 + i % 2, "ds_turned")
             for u in range(2):
-                nc.tensor.transpose(ds_turned[:, u * P : (u + 1) * P], ds_words[:, u * P : (u + 1) * P], ident[:])
+                nc.tensor.transpose(ds_turned[i][:, u * P : (u + 1) * P], ds_words[:, u * P : (u + 1) * P], ident[:])
+
+        def copy_ds(i):
             ds_t[i] = keep.tile([P, N], BF16, name="ds_t%d" % i, tag="ds_t%d" % i, align_bytes=64)
             nc.scalar.copy(
                 out=ds_t[i][:].bitcast(F32).rearrange("s (r u) -> s r u", u=2),
-                in_=ds_turned[:, 0 : 2 * P].rearrange("s (u r) -> s r u", u=2),
+                in_=ds_turned[i][:, 0 : 2 * P].rearrange("s (u r) -> s r u", u=2),
             )
 
         grad = {}
 
         def multiply_keys(i):
             codes, scales = quantize(ds_t[i][:], P, E5M2, "ds%d" % i, pool=ring, tag="dsq")
-            grad[i] = bank(5 + i % 2 if i < TILES - 2 else i % 2, "grad")
+            grad[i] = bank((5, 6, 5, 6, 0, 1, 2, 5)[i], "grad")
             nc.tensor.matmul_mx(
                 out=grad[i][:],
                 lhsT=codes[:].bitcast(E5M2),
@@ -328,26 +340,24 @@ def tile_attend_gat_lse_q_ts_kernel(tc, qT, kT, vT, doT, lse, delta, rw, ts, off
 
         for i in range(2):
             multiply_values(i)
+            cast_do(i + 2, "scalar")
         for i in range(TILES):
             make_ds(i)
-            if i == 0:
-                quantize_do(2, 2, "do2_codes")
-                multiply_values(2)
-            if i == 1:
-                quantize_do(4, 2, "weight0")
-            if i in (3, 4):
-                quantize_do(i + 3, 1, "weight%d" % (i - 1))
-            if i + 3 < TILES:
-                multiply_values(i + 3)
+            if i == 3:
+                cast_do(i + 4, "vector")
+            if i + 2 < TILES:
+                quantize_do(i + 2)
+                multiply_values(i + 2)
             if i >= 2:
                 multiply_keys(i - 2)
+            if i < 3:
+                cast_do(i + 4, "scalar")
+            copy_ds(i)
             if 2 <= i < TILES - 2:
                 store(i - 2, "scalar")
-            if i in (0, 1):
-                cast_do(i + 6, 1, "scalar", "ds%d" % i)
-        multiply_keys(6)
         store(4, "vector")
-        multiply_keys(7)
+        multiply_keys(6)
         store(5, "scalar")
+        multiply_keys(7)
         store(6, "vector")
         store(7, "scalar", parts=2)

@@ -176,21 +176,23 @@ def tile_attend_gat_lse_q_ts_kernel(tc, qT, kT, vT, doT, lse, delta, rw, ts, off
         k_codes, k_scales = quantize(k_bf[:], N, E4M3, "k")
         quantize_signed(0, signed_first)
 
-        def warm_up(target, codes, scales):
+        def warm_up(target, still, fmt, moving):
             nc.tensor.matmul_mx(
                 out=target,
-                lhsT=codes[:, 0:P].bitcast(E4M3),
-                lhsT_scale=scales[:, 0:P],
-                rhs=codes.bitcast(E4M3),
-                rhs_scale=scales,
+                lhsT=still[0][:, 0:P].bitcast(fmt),
+                lhsT_scale=still[1][:, 0:P],
+                rhs=moving[0].bitcast(E4M3),
+                rhs_scale=moving[1],
                 start=True,
                 stop=True,
             )
 
+        ks_half = ks_codes[:, 0 : D // 2], ks_scales[:, 0 : D // 2]
+        k_mx = k_codes[:], k_scales[:]
         for number in (4, 5):
             unread = bank(number, "unread")
             for n in range(2):
-                warm_up(unread[:, n * D // 2 : (n + 1) * D // 2], ks_codes[:, 0 : D // 2], ks_scales[:, 0 : D // 2])
+                warm_up(unread[:, n * D // 2 : (n + 1) * D // 2], ks_half, E4M3, ks_half)
 
         per_half = Q_CHUNK // P
         logits, weights = {}, []
@@ -261,11 +263,12 @@ def tile_attend_gat_lse_q_ts_kernel(tc, qT, kT, vT, doT, lse, delta, rw, ts, off
         weigh(0, (0, 1))
         score(1, q_second)
         weigh(0, (2, 3))
+        warm_up(bank(7, "unread")[:], k_mx, E4M3, k_mx)
         weigh(1, (0, 1))
         cast_do(0, "scalar")
         weigh(1, (2, 3), reuse.tile([P, 2 * N], F32, name="last_weights", align_bytes=64, offset=1024))
         for number in (4, 5):
-            warm_up(bank(number, "unread")[:], k_codes[:], k_scales[:])
+            warm_up(bank(number, "unread")[:], k_mx, E4M3, k_mx)
 
         v_bf = keep.tile([P, PACK * N], BF16, name="v_bf", tag="q_late", align_bytes=64)[:]
         v_places = v_bf.rearrange("p (u s e j) -> p s j u e", u=2, e=2, j=PACK)
@@ -273,6 +276,7 @@ def tile_attend_gat_lse_q_ts_kernel(tc, qT, kT, vT, doT, lse, delta, rw, ts, off
             nc.vector.tensor_copy(out=v_places[:, :, j], in_=v_pool[j][:].indirect(offsets[:]))
 
         quantize_do(0)
+        warm_up(bank(2, "unread")[:], do_mx[0], E5M2, k_mx)
         v_codes = keep.tile([P, N], U32, name="v_codes", align_bytes=64)
         v_scales = reuse.tile([P, N], U8, name="v_scales", align_bytes=64, offset=0)
         nc.vector.quantize_mx(out=v_codes[:].bitcast(E4M3), scales=v_scales[:], in_=v_bf)

@@ -187,12 +187,9 @@ def tile_attend_gat_lse_q_ts_kernel(tc, qT, kT, vT, doT, lse, delta, rw, ts, off
                 stop=True,
             )
 
-        ks_half = ks_codes[:, 0 : D // 2], ks_scales[:, 0 : D // 2]
         k_mx = k_codes[:], k_scales[:]
         for number in (4, 5):
-            unread = bank(number, "unread")
-            for n in range(2):
-                warm_up(unread[:, n * D // 2 : (n + 1) * D // 2], ks_half, E4M3, ks_half)
+            warm_up(bank(number, "unread")[:], k_mx, E4M3, k_mx)
 
         per_half = Q_CHUNK // P
         logits, weights = {}, []
@@ -231,7 +228,7 @@ def tile_attend_gat_lse_q_ts_kernel(tc, qT, kT, vT, doT, lse, delta, rw, ts, off
                 for j in range(PACK):
                     nc.tensor.transpose(turned[:, j * P : (j + 1) * P], logits[half, j][:, m * P : (m + 1) * P], ident[:])
                 if places is None:
-                    weight = keep.tile([P, N], F32, name="weight%d" % i, tag="weight%d" % i, align_bytes=64)
+                    weight = keep.tile([P, N], F32, name="weight%d" % i, tag="v_pool2" if i == per_half else "weight%d" % i, align_bytes=64)
                 else:
                     weight = places[:, m % 2 * N : (m % 2 + 1) * N]
                 nc.scalar.activation(
@@ -263,17 +260,17 @@ def tile_attend_gat_lse_q_ts_kernel(tc, qT, kT, vT, doT, lse, delta, rw, ts, off
         weigh(0, (0, 1))
         score(1, q_second)
         weigh(0, (2, 3))
-        warm_up(bank(7, "unread")[:], k_mx, E4M3, k_mx)
-        weigh(1, (0, 1))
-        cast_do(0, "scalar")
-        weigh(1, (2, 3), reuse.tile([P, 2 * N], F32, name="last_weights", align_bytes=64, offset=1024))
-        for number in (4, 5):
-            warm_up(bank(number, "unread")[:], k_mx, E4M3, k_mx)
-
         v_bf = keep.tile([P, PACK * N], BF16, name="v_bf", tag="q_late", align_bytes=64)[:]
         v_places = v_bf.rearrange("p (u s e j) -> p s j u e", u=2, e=2, j=PACK)
         for j in range(PACK):
             nc.vector.tensor_copy(out=v_places[:, :, j], in_=v_pool[j][:].indirect(offsets[:]))
+
+        weigh(1, (0, 1))
+        cast_do(0, "scalar")
+        weigh(1, (2, 3), reuse.tile([P, 2 * N], F32, name="last_weights", align_bytes=64, offset=1024))
+        unread = bank(4, "unread")
+        for n in range(3):
+            warm_up(unread[:], k_mx, E4M3, k_mx)
 
         quantize_do(0)
         warm_up(bank(2, "unread")[:], do_mx[0], E5M2, k_mx)

@@ -81,7 +81,7 @@ def tile_attend_gat_lse_q_ts_kernel(tc, qT, kT, vT, doT, lse, delta, rw, ts, off
             nc.sync.dma_start(out=rows[TILES * n : TILES * (n + 1), :], in_=vec[0].rearrange("(i m) o -> i (m o)", m=P))
         nc.sync.dma_start(out=ts_pool[0:1, :], in_=ts[0:1, :])
         k_pool.extend(load(k_view[:, j, :], "k_pool%d" % j) for j in range(1, PACK))
-        q_early = load(q_view[:, :, 0:Q_CHUNK], "q_early")
+        q_early = [load(q_view[:, :, n * Q_CHUNK // 2 : (n + 1) * Q_CHUNK // 2], "q_early%d" % n) for n in range(2)]
         q_late = load(q_view[:, :, Q_CHUNK:R], "q_late")
         v_pool = [load(v_view[:, j, :], "v_pool%d" % j) for j in range(PACK)]
         do_first = reuse.tile([P, PACK, P], F32, name="do_first", align_bytes=64, offset=0)
@@ -140,7 +140,7 @@ def tile_attend_gat_lse_q_ts_kernel(tc, qT, kT, vT, doT, lse, delta, rw, ts, off
                 nc.tensor.transpose(turned[:, w * P : (w + 1) * P], words[:, first + w % 2 : first + 2 * P : 2], ident[:])
             return turned
 
-        ks_codes = keep.tile([P, D], U32, name="ks_codes", tag="k_pool3", align_bytes=64)
+        ks_codes = keep.tile([P, D], U32, name="ks_codes", tag="q_early0", align_bytes=64)
         ks_scales = keep.tile([P, D], U8, name="ks_scales", align_bytes=64)
 
         def sign_keys(turned, signed):
@@ -174,7 +174,6 @@ def tile_attend_gat_lse_q_ts_kernel(tc, qT, kT, vT, doT, lse, delta, rw, ts, off
         interleave_keys(1)
         k_turned = turn_keys(1, 7)
         k_codes, k_scales = quantize(k_bf[:], N, E4M3, "k")
-        quantize_signed(0, signed_first)
 
         def warm_up(target, still, fmt, moving):
             nc.tensor.matmul_mx(
@@ -188,8 +187,6 @@ def tile_attend_gat_lse_q_ts_kernel(tc, qT, kT, vT, doT, lse, delta, rw, ts, off
             )
 
         k_mx = k_codes[:], k_scales[:]
-        for number in (4, 5):
-            warm_up(bank(number, "unread")[:], k_mx, E4M3, k_mx)
 
         per_half = Q_CHUNK // P
         logits, weights = {}, []
@@ -241,19 +238,16 @@ def tile_attend_gat_lse_q_ts_kernel(tc, qT, kT, vT, doT, lse, delta, rw, ts, off
 
         quarter = Q_CHUNK // 2
         q_first = (
-            keep.tile([P, Q_CHUNK], U32, name="q0_codes", tag="q_early", align_bytes=64),
+            keep.tile([P, Q_CHUNK], U32, name="q0_codes", align_bytes=64),
             keep.tile([P, Q_CHUNK], U8, name="q0_scales", align_bytes=64),
         )
-        parts_q = [slice(n * quarter, (n + 1) * quarter) for n in range(2)]
-        q_bf0 = [
-            interleave(q_early[:, :, part], (engine,), "q_bf0_%s" % engine, "q_bf0_%s" % engine)
-            for part, engine in zip(parts_q, ("scalar", "vector"))
-        ]
-        for part, grouped in zip(parts_q, q_bf0):
+        for n, engine in enumerate(("scalar", "vector")):
+            part = slice(n * quarter, (n + 1) * quarter)
+            grouped = interleave(q_early[n], (engine,), "q_bf0_%s" % engine, "q_bf0")
             nc.vector.quantize_mx(out=q_first[0][:, part].bitcast(E4M3), scales=q_first[1][:, part], in_=grouped[:])
-        for part in parts_q:
             score(0, q_first, part)
-        signed_second = sign_keys(k_turned, keep.tile([P, 2 * N], BF16, name="signed1", tag="q_bf0_scalar", align_bytes=64))
+        quantize_signed(0, signed_first)
+        signed_second = sign_keys(k_turned, keep.tile([P, 2 * N], BF16, name="signed1", tag="q_early1", align_bytes=64))
         q_bf1 = interleave(q_late, ("vector",), "q_bf1", "q_bf1")
         q_second = quantize(q_bf1[:], Q_CHUNK, E4M3, "q1")
         quantize_signed(1, signed_second)

@@ -72,8 +72,10 @@ def tile_attend_gat_lse_q_ts_kernel(tc, qT, kT, vT, doT, lse, delta, rw, ts, off
         nc.gpsimd.memset(ts_pool[:, T // 2 : T], 0.0)
         ident = keep.tile([P, P], F32, name="ident")
         make_identity(nc, ident[:])
+        one = keep.tile([P, 1], F32, name="one")
+        nc.vector.memset(one[:], 1.0)
         warm_ln = keep.tile([P, 1], F32, name="warm_ln")
-        nc.scalar.activation(warm_ln[:], ident[:, 0:1], ACT.Ln, bias=1.0)
+        nc.scalar.activation(warm_ln[:], one[:], ACT.Ln)
 
         k_pool = [load(k_view[:, 0, :], "k_pool0")]
         nc.sync.dma_start(offsets[:], offs)
@@ -119,7 +121,7 @@ def tile_attend_gat_lse_q_ts_kernel(tc, qT, kT, vT, doT, lse, delta, rw, ts, off
         nc.scalar.copy(out=cols[:, 0:4], in_=ts_cols)
         ts_sign = keep.tile([P, 2, PACK], BF16, name="ts_sign")
         nc.scalar.activation(ts_sign[:], ts_cols.unsqueeze(1).to_broadcast([P, 2, PACK]), ACT.Sign)
-        parts = keep.tile([P, 3, 12], F32, name="parts")
+        parts = keep.tile([P, 3, 12], F32, name="parts", tag="parts")
         nc.gpsimd.tensor_scalar(parts[:, 0, :], absolute[:], 2.0**64, 2.0**-63, ALU.min, ALU.max)
         nc.gpsimd.tensor_scalar(parts[:, 1, :], absolute[:], 2.0**-64, 1.0, ALU.mult, ALU.max)
         nc.gpsimd.tensor_scalar(parts[:, 2, :], absolute[:], 2.0**-63, 2.0**-126, ALU.min, ALU.max)
@@ -129,8 +131,8 @@ def tile_attend_gat_lse_q_ts_kernel(tc, qT, kT, vT, doT, lse, delta, rw, ts, off
         nc.gpsimd.tensor_tensor(sums[:], terms[:, 0:2, :], terms[:, 2:4, :], ALU.add)
         shift = keep.tile([P, 12], F32, name="shift", tag="shift", align_bytes=64)
         nc.gpsimd.tensor_tensor(shift[:], sums[:, 0, :], sums[:, 1, :], ALU.add)
-        warm = keep.tile([P, 1], F32, name="warm")
-        nc.scalar.activation(warm[:], terms[:, 2, 0:1], ACT.Exp)
+        warm = keep.tile([P, 1], F32, name="warm", tag="parts")
+        nc.scalar.activation(warm[:], one[:], ACT.Exp)
 
         def turn_keys(a, number):
             words = k_pairs[a][:].bitcast(F32)
@@ -263,7 +265,7 @@ def tile_attend_gat_lse_q_ts_kernel(tc, qT, kT, vT, doT, lse, delta, rw, ts, off
         cast_do(0, "scalar")
         weigh(1, (2, 3), reuse.tile([P, 2 * N], F32, name="last_weights", align_bytes=64, offset=1024))
         unread = bank(4, "unread")
-        for n in range(3):
+        for n in range(2):
             warm_up(unread[:], k_mx, E4M3, k_mx)
 
         quantize_do(0)
@@ -336,6 +338,7 @@ def tile_attend_gat_lse_q_ts_kernel(tc, qT, kT, vT, doT, lse, delta, rw, ts, off
         for i in range(2):
             multiply_values(i)
             cast_do(i + 2, "scalar")
+        warm_up(bank(4, "unread")[:], do_mx[1], E5M2, (v_codes[:], v_scales[:]))
         for i in range(TILES):
             make_ds(i)
             if i == 3:

@@ -34,8 +34,8 @@ def tile_attend_gat_lse_q_ts_kernel(tc, qT, kT, vT, doT, lse, delta, rw, ts, off
         def bank(number, name):
             return psum.tile([P, 512], F32, name=name, tag="bank%d" % number)
 
-        def quantize(src, width, fmt, name, pool=keep, tag=None):
-            codes = pool.tile([P, width], U32, name=name + "_codes", tag=(tag or name) + "_codes", align_bytes=64)
+        def quantize(src, width, fmt, name, pool=keep, tag=None, held=None):
+            codes = pool.tile([P, width], U32, name=name + "_codes", tag=held or (tag or name) + "_codes", align_bytes=64)
             scales = pool.tile([P, width], U8, name=name + "_scales", tag=(tag or name) + "_scales", align_bytes=64)
             nc.vector.quantize_mx(out=codes[:].bitcast(fmt), scales=scales[:], in_=src)
             return codes, scales
@@ -217,8 +217,8 @@ def tile_attend_gat_lse_q_ts_kernel(tc, qT, kT, vT, doT, lse, delta, rw, ts, off
         def cast_do(i, engine, tag=None):
             do_bf[i] = interleave(do_raw[i], (engine,), "do_bf%d" % i, tag or "do_bf%d" % i)
 
-        def quantize_do(i):
-            do_mx[i] = quantize(do_bf[i][:], P, E5M2, "do%d" % i)
+        def quantize_do(i, held=None):
+            do_mx[i] = quantize(do_bf[i][:], P, E5M2, "do%d" % i, held=held)
 
         def weigh(half, members, places=None):
             for m in members:
@@ -229,7 +229,7 @@ def tile_attend_gat_lse_q_ts_kernel(tc, qT, kT, vT, doT, lse, delta, rw, ts, off
                 if places is None:
                     weight = keep.tile([P, N], F32, name="weight%d" % i, tag="v_pool2" if i == per_half else "weight%d" % i, align_bytes=64)
                 else:
-                    weight = places[:, m % 2 * N : (m % 2 + 1) * N]
+                    weight = places
                 nc.scalar.activation(
                     weight[:].rearrange("p (u s e) -> p u s e", u=2, e=2),
                     turned[:].rearrange("p (u e s) -> p u s e", u=2, e=2),
@@ -263,10 +263,8 @@ def tile_attend_gat_lse_q_ts_kernel(tc, qT, kT, vT, doT, lse, delta, rw, ts, off
 
         weigh(1, (0, 1))
         cast_do(0, "scalar")
-        weigh(1, (2, 3), reuse.tile([P, 2 * N], F32, name="last_weights", align_bytes=64, offset=1024))
-        unread = bank(4, "unread")
-        for n in range(2):
-            warm_up(unread[:], k_mx, E4M3, k_mx)
+        weigh(1, (2,), reuse.tile([P, N], F32, name="seventh_weights", align_bytes=64, offset=1024))
+        warm_up(bank(5, "unread")[:], k_mx, E4M3, k_mx)
 
         quantize_do(0)
         warm_up(bank(2, "unread")[:], do_mx[0], E5M2, k_mx)
@@ -280,7 +278,7 @@ def tile_attend_gat_lse_q_ts_kernel(tc, qT, kT, vT, doT, lse, delta, rw, ts, off
 
         def multiply_values(i):
             codes, scales = do_mx[i]
-            dp[i] = bank((0, 1, 2, 7)[i % 4], "dp")
+            dp[i] = bank((0, 1, 2, 6)[i % 4], "dp")
             nc.tensor.matmul_mx(
                 out=dp[i][:],
                 lhsT=codes[:].bitcast(E5M2),
@@ -294,7 +292,7 @@ def tile_attend_gat_lse_q_ts_kernel(tc, qT, kT, vT, doT, lse, delta, rw, ts, off
         ds_turned = {}
 
         def make_ds(i):
-            ds = keep.tile([P, N], BF16, name="ds%d" % i, tag="ds%d" % i, align_bytes=64)
+            ds = keep.tile([P, N], BF16, name="ds%d" % i, tag="ds_t%d" % (i - 3) if 3 <= i < 6 else "ds%d" % i, align_bytes=64)
             nc.vector.scalar_tensor_tensor(ds[:], dp[i][:], cols[:, 4 + i : 5 + i], weights[i][:], ALU.subtract, ALU.mult)
             ds_words = ds[:].bitcast(F32)
             ds_turned[i] = bank(3 + i % 2, "ds_turned")
@@ -308,11 +306,12 @@ def tile_attend_gat_lse_q_ts_kernel(tc, qT, kT, vT, doT, lse, delta, rw, ts, off
                 in_=ds_turned[i][:, 0 : 2 * P].rearrange("s (u r) -> s r u", u=2),
             )
 
-        grad = {}
+        grad, ds_mx = {}, {}
 
         def multiply_keys(i):
             codes, scales = quantize(ds_t[i][:], P, E5M2, "ds%d" % i, pool=ring, tag="dsq")
-            grad[i] = bank((5, 6, 5, 6, 0, 1, 2, 5)[i], "grad")
+            ds_mx[i] = codes, scales
+            grad[i] = bank((5, 7, 5, 7, 0, 2, 6, 5)[i], "grad")
             nc.tensor.matmul_mx(
                 out=grad[i][:],
                 lhsT=codes[:].bitcast(E5M2),
@@ -335,24 +334,32 @@ def tile_attend_gat_lse_q_ts_kernel(tc, qT, kT, vT, doT, lse, delta, rw, ts, off
                     nc.scalar.activation(ordered, halves, ACT.Copy, scale=rw_sign[:, i : i + 1])
                 nc.sync.dma_start(out=out[0, i * P : (i + 1) * P, n * width : (n + 1) * width], in_=result[:])
 
-        for i in range(2):
+        cast_do(2, "scalar")
+        weigh(1, (3,), keep.tile([P, N], F32, name="last_weights", tag="do_raw1", align_bytes=64))
+        quantize_do(2)
+        for i in range(3):
             multiply_values(i)
-            cast_do(i + 2, "scalar")
-        warm_up(bank(4, "unread")[:], do_mx[1], E5M2, (v_codes[:], v_scales[:]))
+        cast_do(4, "scalar")
         for i in range(TILES):
             make_ds(i)
-            if i == 3:
-                cast_do(i + 4, "vector")
-            if i + 2 < TILES:
-                quantize_do(i + 2)
-                multiply_values(i + 2)
+            if i == 0:
+                cast_do(3, "vector", "weight0")
             if i >= 2:
                 multiply_keys(i - 2)
-            if i < 3:
-                cast_do(i + 4, "scalar")
+            if i + 3 < TILES:
+                quantize_do(i + 3, "weight1" if i == 1 else None)
+                multiply_values(i + 3)
+            if i == 0:
+                warm_up(bank(5, "unread")[:], do_mx[3], E5M2, (v_codes[:], v_scales[:]))
+            if i == 5:
+                warm_up(bank(1, "unread")[:], ds_mx[3], E5M2, (ks_codes[:], ks_scales[:]))
             copy_ds(i)
             if 2 <= i < TILES - 2:
                 store(i - 2, "scalar")
+            if i < 2:
+                cast_do(i + 5, "scalar", "ds%d" % i)
+            if i == 2:
+                cast_do(TILES - 1, "vector", "ds2")
         store(4, "vector")
         multiply_keys(6)
         store(5, "scalar")

@@ -264,7 +264,9 @@ def tile_attend_gat_lse_q_ts_kernel(tc, qT, kT, vT, doT, lse, delta, rw, ts, off
         weigh(1, (0, 1))
         cast_do(0, "scalar")
         weigh(1, (2,), reuse.tile([P, N], F32, name="seventh_weights", align_bytes=64, offset=1024))
-        warm_up(bank(5, "unread")[:], k_mx, E4M3, k_mx)
+        unread = bank(5, "unread")
+        for n in range(2):
+            warm_up(unread[:], k_mx, E4M3, k_mx)
 
         quantize_do(0)
         warm_up(bank(2, "unread")[:], do_mx[0], E5M2, k_mx)
@@ -349,8 +351,6 @@ def tile_attend_gat_lse_q_ts_kernel(tc, qT, kT, vT, doT, lse, delta, rw, ts, off
             if i + 3 < TILES:
                 quantize_do(i + 3, "weight1" if i == 1 else None)
                 multiply_values(i + 3)
-            if i == 0:
-                warm_up(bank(5, "unread")[:], do_mx[3], E5M2, (v_codes[:], v_scales[:]))
             if i == 5:
                 warm_up(bank(1, "unread")[:], ds_mx[3], E5M2, (ks_codes[:], ks_scales[:]))
             copy_ds(i)

@@ -264,9 +264,7 @@ def tile_attend_gat_lse_q_ts_kernel(tc, qT, kT, vT, doT, lse, delta, rw, ts, off
         weigh(1, (0, 1))
         cast_do(0, "scalar")
         weigh(1, (2,), reuse.tile([P, N], F32, name="seventh_weights", align_bytes=64, offset=1024))
-        unread = bank(5, "unread")
-        for n in range(2):
-            warm_up(unread[:], k_mx, E4M3, k_mx)
+        warm_up(bank(5, "unread")[:], k_mx, E4M3, k_mx)
 
         quantize_do(0)
         warm_up(bank(2, "unread")[:], do_mx[0], E5M2, k_mx)
@@ -341,16 +339,17 @@ def tile_attend_gat_lse_q_ts_kernel(tc, qT, kT, vT, doT, lse, delta, rw, ts, off
         quantize_do(2)
         for i in range(3):
             multiply_values(i)
+        cast_do(3, "scalar")
         cast_do(4, "scalar")
         for i in range(TILES):
             make_ds(i)
-            if i == 0:
-                cast_do(3, "vector", "weight0")
             if i >= 2:
                 multiply_keys(i - 2)
             if i + 3 < TILES:
-                quantize_do(i + 3, "weight1" if i == 1 else None)
+                quantize_do(i + 3, "weight%d" % i if i < 2 else None)
                 multiply_values(i + 3)
+            if i < 2:
+                warm_up(bank(5, "unread")[:, 0 : N // 2], do_mx[i + 3], E5M2, (v_codes[:, 0 : N // 2], v_scales[:, 0 : N // 2]))
             if i == 5:
                 warm_up(bank(1, "unread")[:], ds_mx[3], E5M2, (ks_codes[:], ks_scales[:]))
             copy_ds(i)

from contextlib import ExitStack

import concourse.mybir as mybir
from concourse.masks import make_identity

N, T, D, DV, R = 512, 2048, 512, 512, 1024
FLOPS = 2 * R * N * (D + DV + D)

F32 = mybir.dt.float32
BF16 = mybir.dt.bfloat16
U32 = mybir.dt.uint32
U16 = mybir.dt.uint16
U8 = mybir.dt.uint8
E4M3 = mybir.dt.float8_e4m3fn_x4
E5M2 = mybir.dt.float8_e5m2_x4
ALU = mybir.AluOpType
ACT = mybir.ActivationFunctionType

P = 128
PACK = 4
TILES = R // P
Q_CHUNK = 512
DO_LOADS = ((1, 2), (3, 2), (5, 2), (7, 1))


def tile_attend_gat_lse_q_ts_kernel(tc, qT, kT, vT, doT, lse, delta, rw, ts, offs, out):
    nc = tc.nc
    with ExitStack() as ctx:
        keep = ctx.enter_context(tc.tile_pool(name="keep", bufs=1))
        ring = ctx.enter_context(tc.tile_pool(name="ring", bufs=4))
        reuse = ctx.enter_context(tc.tile_pool(name="reuse", bufs=1))
        psum = ctx.enter_context(tc.psum_pool(name="psum", bufs=1))

        def bank(number, name):
            return psum.tile([P, 512], F32, name=name, tag="bank%d" % number)

        def quantize(src, width, fmt, name, pool=keep, tag=None, held=None):
            codes = pool.tile([P, width], U32, name=name + "_codes", tag=held or (tag or name) + "_codes", align_bytes=64)
            scales = pool.tile([P, width], U8, name=name + "_scales", tag=(tag or name) + "_scales", align_bytes=64)
            nc.vector.quantize_mx(out=codes[:].bitcast(fmt), scales=scales[:], in_=src)
            return codes, scales

        def interleave(raw, engines, name, tag, grouped=None):
            width = raw.shape[2]
            share = width // len(engines)
            if grouped is None:
                grouped = keep.tile([P, width * PACK], BF16, name=name, tag=tag, align_bytes=64)
            for n, engine in enumerate(engines):
                dst = grouped[:, n * share * PACK : (n + 1) * share * PACK].rearrange("p (c i j) -> p c j i", i=4, j=PACK)
                src = raw[:, :, n * share : (n + 1) * share].rearrange("p j (c i) -> p c j i", i=4)
                if engine == "vector":
                    nc.vector.tensor_copy(out=dst, in_=src)
                else:
                    nc.scalar.copy(out=dst, in_=src)
            return grouped

        offsets = keep.tile([P, N // 16], U16, name="offsets")
        q_view = qT[0].rearrange("(p j) r -> p j r", j=PACK)
        do_view = doT[0].rearrange("(p j) r -> p j r", j=PACK)
        k_view = kT.rearrange("(p j) t -> p j t", j=PACK)
        v_view = vT.rearrange("(p j) t -> p j t", j=PACK)

        def load(view, name):
            raw = keep.tile(list(view.shape), F32, name=name, tag=name, align_bytes=64)
            nc.sync.dma_start(out=raw[:], in_=view)
            return raw

        rows = keep.tile([P, P], F32, name="rows")
        nc.vector.memset(rows[:], 0.0)
        ts_pool = keep.tile([P, T], F32, name="ts_pool")
        nc.vector.memset(ts_pool[:, 0 : T // 2], 0.0)
        nc.gpsimd.memset(ts_pool[:, T // 2 : T], 0.0)
        ident = keep.tile([P, P], F32, name="ident")
        make_identity(nc, ident[:])
        one = keep.tile([P, 1], F32, name="one")
        nc.vector.memset(one[:], 1.0)
        warm_ln = keep.tile([P, 1], F32, name="warm_ln")
        nc.scalar.activation(warm_ln[:], one[:], ACT.Ln)

        k_pool = [load(k_view[:, 0, :], "k_pool0")]
        nc.sync.dma_start(offsets[:], offs)
        for n, vec in enumerate((rw, delta, lse)):
            nc.sync.dma_start(out=rows[TILES * n : TILES * (n + 1), :], in_=vec[0].rearrange("(i m) o -> i (m o)", m=P))
        nc.sync.dma_start(out=ts_pool[0:1, :], in_=ts[0:1, :])
        k_pool.extend(load(k_view[:, j, :], "k_pool%d" % j) for j in range(1, PACK))
        q_early = [load(q_view[:, :, n * Q_CHUNK // 2 : (n + 1) * Q_CHUNK // 2], "q_early%d" % n) for n in range(2)]
        q_late = load(q_view[:, :, Q_CHUNK:R], "q_late")
        v_pool = [load(v_view[:, j, :], "v_pool%d" % j) for j in range(PACK)]
        do_first = reuse.tile([P, PACK, P], F32, name="do_first", align_bytes=64, offset=0)
        nc.sync.dma_start(out=do_first[:], in_=do_view[:, :, 0:P])
        do_raw = {0: do_first}
        for first, count in DO_LOADS:
            raw = load(do_view[:, :, first * P : (first + count) * P], "do_raw%d" % first)
            for n in range(count):
                do_raw[first + n] = raw[:, :, n * P : (n + 1) * P]

        k_pairs = [keep.tile([P, 2 * N], BF16, name="k_pair%d" % a, align_bytes=64) for a in range(2)]

        def gather_keys(j):
            nc.vector.tensor_copy(out=k_pairs[j // 2][:, j % 2 * N : (j % 2 + 1) * N], in_=k_pool[j][:].indirect(offsets[:]))

        gather_keys(0)

        ts_row = keep.tile([P, N], F32, name="ts_row")
        nc.vector.tensor_copy(out=ts_row[:], in_=ts_pool[:].indirect(offsets[:]))
        ts_by_place = bank(0, "ts_by_place")
        rows_t = bank(1, "rows_t")
        nc.tensor.transpose(rows_t[:, 0:P], rows[:], ident[:])
        for t in range(PACK):
            nc.tensor.transpose(ts_by_place[:, t * P : (t + 1) * P], ts_row[:, t:N:PACK], ident[:])
        ts_cols = ts_by_place[:, 0:N:P]
        absolute = keep.tile([P, 12], F32, name="absolute")
        nc.scalar.activation(absolute[:, 0:8], rows_t[:, 0:8], ACT.Abs)
        rw_sign = keep.tile([P, TILES], F32, name="rw_sign")
        nc.scalar.activation(rw_sign[:], rows_t[:, 0:8], ACT.Sign)
        cols = keep.tile([P, 12], F32, name="cols")
        nc.scalar.copy(out=cols[:, 4:12], in_=rows_t[:, 8:16])
        terms = keep.tile([P, 4, 12], F32, name="terms", tag="terms", align_bytes=64)
        nc.scalar.activation(terms[:, 3, :], rows_t[:, 16:28], ACT.Copy, scale=-1.0)
        nc.scalar.activation(absolute[:, 8:12], ts_cols, ACT.Abs)
        nc.scalar.copy(out=cols[:, 0:4], in_=ts_cols)
        ts_sign = keep.tile([P, 2, PACK], BF16, name="ts_sign")
        nc.scalar.activation(ts_sign[:], ts_cols.unsqueeze(1).to_broadcast([P, 2, PACK]), ACT.Sign)
        parts = keep.tile([P, 3, 12], F32, name="parts", tag="parts")
        nc.gpsimd.tensor_scalar(parts[:, 0, :], absolute[:], 2.0**64, 2.0**-63, ALU.min, ALU.max)
        nc.gpsimd.tensor_scalar(parts[:, 1, :], absolute[:], 2.0**-64, 1.0, ALU.mult, ALU.max)
        nc.gpsimd.tensor_scalar(parts[:, 2, :], absolute[:], 2.0**-63, 2.0**-126, ALU.min, ALU.max)
        nc.scalar.activation(terms[:, 0:2, :], parts[:, 0:2, :], ACT.Ln)
        nc.scalar.activation(terms[:, 2, :], parts[:, 2, :], ACT.Ln, scale=2.0**63)
        sums = keep.tile([P, 2, 12], F32, name="sums")
        nc.gpsimd.tensor_tensor(sums[:], terms[:, 0:2, :], terms[:, 2:4, :], ALU.add)
        shift = keep.tile([P, 12], F32, name="shift", tag="shift", align_bytes=64)
        nc.gpsimd.tensor_tensor(shift[:], sums[:, 0, :], sums[:, 1, :], ALU.add)
        warm = keep.tile([P, 1], F32, name="warm", tag="parts")
        nc.scalar.activation(warm[:], one[:], ACT.Exp)

        def turn_keys(a, number):
            words = k_pairs[a][:].bitcast(F32)
            turned = bank(number, "k_turned")
            for w in range(4):
                first = 2 * P * (w // 2)
                nc.tensor.transpose(turned[:, w * P : (w + 1) * P], words[:, first + w % 2 : first + 2 * P : 2], ident[:])
            return turned

        ks_codes = keep.tile([P, D], U32, name="ks_codes", tag="q_early0", align_bytes=64)
        ks_scales = keep.tile([P, D], U8, name="ks_scales", align_bytes=64)

        def sign_keys(turned, signed):
            nc.vector.tensor_tensor(
                signed[:].rearrange("s (p w e) -> s p w e", w=4, e=2),
                turned[:].bitcast(BF16).rearrange("s (w p e) -> s p w e", w=4, e=2),
                ts_sign[:].rearrange("s j (u e) -> s (j u) e", e=2).unsqueeze(1).to_broadcast([P, P, 4, 2]),
                ALU.mult,
            )
            return signed

        def quantize_signed(a, signed):
            part = slice(a * D // 2, (a + 1) * D // 2)
            nc.vector.quantize_mx(out=ks_codes[:, part].bitcast(E4M3), scales=ks_scales[:, part], in_=signed[:])

        k_bf = keep.tile([P, N * PACK], BF16, name="k_bf", tag="k_bf", align_bytes=64)

        def interleave_keys(a):
            nc.vector.tensor_copy(
                out=k_bf[:].rearrange("p (t s j) -> p s j t", t=PACK, j=PACK)[:, :, 2 * a : 2 * a + 2, :],
                in_=k_pairs[a][:].rearrange("p (j s t) -> p s j t", j=2, t=PACK),
            )

        last = PACK - 1
        gather_keys(1)
        k_turned = turn_keys(0, 6)
        interleave_keys(0)
        gather_keys(2)
        signed_first = sign_keys(k_turned, keep.tile([P, 2 * N], BF16, name="signed0", tag="k_pool2", align_bytes=64))
        gather_keys(3)
        interleave_keys(1)
        k_turned = turn_keys(1, 7)
        k_codes, k_scales = quantize(k_bf[:], N, E4M3, "k")

        def warm_up(target, still, fmt, moving):
            nc.tensor.matmul_mx(
                out=target,
                lhsT=still[0][:, 0:P].bitcast(fmt),
                lhsT_scale=still[1][:, 0:P],
                rhs=moving[0].bitcast(E4M3),
                rhs_scale=moving[1],
                start=True,
                stop=True,
            )

        k_mx = k_codes[:], k_scales[:]

        per_half = Q_CHUNK // P
        logits, weights = {}, []

        def score(half, q_mx, rows_in=slice(0, Q_CHUNK)):
            q_codes, q_scales = q_mx
            for j in range(PACK):
                scores = bank(j, "scores")
                nc.tensor.matmul_mx(
                    out=scores[:, rows_in],
                    lhsT=k_codes[:, j * P : (j + 1) * P].bitcast(E4M3),
                    lhsT_scale=k_scales[:, j * P : (j + 1) * P],
                    rhs=q_codes[:, rows_in].bitcast(E4M3),
                    rhs_scale=q_scales[:, rows_in],
                    start=True,
                    stop=True,
                )
                if (half, j) not in logits:
                    logits[half, j] = keep.tile([P, Q_CHUNK], F32, name="logit%d_%d" % (half, j), tag="logit%d_%d" % (half, j), align_bytes=64)
                nc.scalar.activation(
                    logits[half, j][:, rows_in], scores[:, rows_in], ACT.Identity, bias=shift[:, 8 + j : 9 + j], scale=cols[:, j : j + 1]
                )

        do_mx, do_bf = {}, {}

        def cast_do(i, engine, tag=None):
            do_bf[i] = interleave(do_raw[i], (engine,), "do_bf%d" % i, tag or "do_bf%d" % i)

        def quantize_do(i, held=None):
            do_mx[i] = quantize(do_bf[i][:], P, E5M2, "do%d" % i, held=held)

        def weigh(half, members, places=None):
            for m in members:
                i = half * per_half + m
                turned = bank(4 + m, "turned")
                for j in range(PACK):
                    nc.tensor.transpose(turned[:, j * P : (j + 1) * P], logits[half, j][:, m * P : (m + 1) * P], ident[:])
                if places is None:
                    weight = keep.tile([P, N], F32, name="weight%d" % i, tag="v_pool2" if i == per_half else "weight%d" % i, align_bytes=64)
                else:
                    weight = places
                nc.scalar.activation(
                    weight[:].rearrange("p (u s e) -> p u s e", u=2, e=2),
                    turned[:].rearrange("p (u e s) -> p u s e", u=2, e=2),
                    ACT.Exp,
                    bias=shift[:, i : i + 1],
                )
                weights.append(weight)

        quarter = Q_CHUNK // 2
        q_first = (
            keep.tile([P, Q_CHUNK], U32, name="q0_codes", align_bytes=64),
            keep.tile([P, Q_CHUNK], U8, name="q0_scales", align_bytes=64),
        )
        for n, engine in enumerate(("scalar", "vector")):
            part = slice(n * quarter, (n + 1) * quarter)
            grouped = interleave(q_early[n], (engine,), "q_bf0_%s" % engine, "q_bf0")
            nc.vector.quantize_mx(out=q_first[0][:, part].bitcast(E4M3), scales=q_first[1][:, part], in_=grouped[:])
            score(0, q_first, part)
        quantize_signed(0, signed_first)
        signed_second = sign_keys(k_turned, keep.tile([P, 2 * N], BF16, name="signed1", tag="q_early1", align_bytes=64))
        q_bf1 = interleave(q_late, ("vector",), "q_bf1", "q_bf1")
        q_second = quantize(q_bf1[:], Q_CHUNK, E4M3, "q1")
        quantize_signed(1, signed_second)
        weigh(0, (0, 1))
        score(1, q_second)
        weigh(0, (2, 3))
        v_bf = keep.tile([P, PACK * N], BF16, name="v_bf", tag="q_late", align_bytes=64)[:]
        v_places = v_bf.rearrange("p (u s e j) -> p s j u e", u=2, e=2, j=PACK)
        for j in range(PACK):
            nc.vector.tensor_copy(out=v_places[:, :, j], in_=v_pool[j][:].indirect(offsets[:]))

        weigh(1, (0, 1))
        cast_do(0, "scalar")
        weigh(1, (2,), reuse.tile([P, N], F32, name="seventh_weights", align_bytes=64, offset=1024))
        warm_up(bank(5, "unread")[:], k_mx, E4M3, k_mx)

        quantize_do(0)
        warm_up(bank(2, "unread")[:], do_mx[0], E5M2, k_mx)
        v_codes = keep.tile([P, N], U32, name="v_codes", align_bytes=64)
        v_scales = reuse.tile([P, N], U8, name="v_scales", align_bytes=64, offset=0)
        nc.vector.quantize_mx(out=v_codes[:].bitcast(E4M3), scales=v_scales[:], in_=v_bf)
        cast_do(1, "vector")
        quantize_do(1)

        dp, ds_t = {}, {}

        def multiply_values(i):
            codes, scales = do_mx[i]
            dp[i] = bank((0, 1, 2, 6)[i % 4], "dp")
            nc.tensor.matmul_mx(
                out=dp[i][:],
                lhsT=codes[:].bitcast(E5M2),
                lhsT_scale=scales[:],
                rhs=v_codes[:].bitcast(E4M3),
                rhs_scale=v_scales[:],
                start=True,
                stop=True,
            )

        ds_turned = {}

        def make_ds(i):
            ds = keep.tile([P, N], BF16, name="ds%d" % i, tag="ds_t%d" % (i - 3) if 3 <= i < 6 else "ds%d" % i, align_bytes=64)
            nc.vector.scalar_tensor_tensor(ds[:], dp[i][:], cols[:, 4 + i : 5 + i], weights[i][:], ALU.subtract, ALU.mult)
            ds_words = ds[:].bitcast(F32)
            ds_turned[i] = bank(3 + i % 2, "ds_turned")
            for u in range(2):
                nc.tensor.transpose(ds_turned[i][:, u * P : (u + 1) * P], ds_words[:, u * P : (u + 1) * P], ident[:])

        def copy_ds(i):
            ds_t[i] = keep.tile([P, N], BF16, name="ds_t%d" % i, tag="ds_t%d" % i, align_bytes=64)
            nc.scalar.copy(
                out=ds_t[i][:].bitcast(F32).rearrange("s (r u) -> s r u", u=2),
                in_=ds_turned[i][:, 0 : 2 * P].rearrange("s (u r) -> s r u", u=2),
            )

        grad, ds_mx = {}, {}

        def multiply_keys(i):
            codes, scales = quantize(ds_t[i][:], P, E5M2, "ds%d" % i, pool=ring, tag="dsq")
            ds_mx[i] = codes, scales
            grad[i] = bank((5, 7, 5, 7, 0, 2, 6, 5)[i], "grad")
            nc.tensor.matmul_mx(
                out=grad[i][:],
                lhsT=codes[:].bitcast(E5M2),
                lhsT_scale=scales[:],
                rhs=ks_codes[:].bitcast(E4M3),
                rhs_scale=ks_scales[:],
                start=True,
                stop=True,
            )

        def store(i, engine, parts=1):
            width = D // parts
            for n in range(parts):
                result = keep.tile([P, width], F32, name="result%d_%d" % (i, n))
                ordered = result[:].rearrange("r (p a j) -> r p a j", a=2, j=2)
                halves = grad[i][:].rearrange("r (a p j) -> r p a j", a=2, j=2)[:, n * width // PACK : (n + 1) * width // PACK]
                if engine == "vector":
                    nc.vector.tensor_scalar(ordered, halves, rw_sign[:, i : i + 1], None, ALU.mult)
                else:
                    nc.scalar.activation(ordered, halves, ACT.Copy, scale=rw_sign[:, i : i + 1])
                nc.sync.dma_start(out=out[0, i * P : (i + 1) * P, n * width : (n + 1) * width], in_=result[:])

        cast_do(2, "scalar")
        weigh(1, (3,), keep.tile([P, N], F32, name="last_weights", tag="do_raw1", align_bytes=64))
        quantize_do(2)
        for i in range(3):
            multiply_values(i)
        cast_do(3, "scalar")
        cast_do(4, "scalar")
        for i in range(TILES):
            make_ds(i)
            if i >= 2:
                multiply_keys(i - 2)
            if i + 3 < TILES:
                quantize_do(i + 3, "weight%d" % i if i < 2 else None)
                multiply_values(i + 3)
            if i < 2:
                warm_up(bank(5, "unread")[:, 0 : N // 2], do_mx[i + 3], E5M2, (v_codes[:, 0 : N // 2], v_scales[:, 0 : N // 2]))
            if i == 5:
                warm_up(bank(1, "unread")[:], ds_mx[3], E5M2, (ks_codes[:], ks_scales[:]))
            copy_ds(i)
            if 2 <= i < TILES - 2:
                store(i - 2, "scalar")
            if i < 2:
                cast_do(i + 5, "scalar", "ds%d" % i)
            if i == 2:
                cast_do(TILES - 1, "vector", "ds2")
        store(4, "vector")
        multiply_keys(6)
        store(5, "scalar")
        multiply_keys(7)
        store(6, "vector")
        store(7, "scalar", parts=2)
